import numpy as np
import ml_dtypes


def mxq(x, axis, fmt="e4m3"):
    dtype, down = {"e4m3": (ml_dtypes.float8_e4m3fn, 7), "e5m2": (ml_dtypes.float8_e5m2, 14)}[fmt]
    v = np.moveaxis(np.asarray(x, np.float32).astype(ml_dtypes.bfloat16).astype(np.float64), axis, -1)
    blocks = v.reshape(v.shape[:-1] + (-1, 32))
    amax = np.abs(blocks).max(-1, keepdims=True)
    byte = np.maximum(np.where(amax > 0, np.frexp(amax)[1] - 1 + 127, 0) - down, 1)
    scale = np.exp2(byte - 127.0)
    codes = (blocks / scale).astype(np.float32).astype(dtype).astype(np.float64)
    return np.moveaxis((codes * scale).reshape(v.shape), -1, axis)


WIDE = False


def mx_kscale(k):
    if not WIDE:
        return np.ones(k)
    levels = np.array([10, -10, 5, -5, 0])
    if k % 512:
        return np.exp2(np.random.permutation(np.resize(levels, k // 32))).repeat(32)
    a = np.empty((k // 512, 16))
    for p in range(k // 512):
        a[p, :8] = np.random.permutation(np.resize(levels, 8))
        for g in range(8):
            far = levels[np.abs(levels - a[p, g]) >= 10]
            a[p, g + 8] = far[np.random.randint(len(far))]
    return np.exp2(a.ravel()).repeat(32)


def f64(x):
    return np.asarray(x).astype(np.float64)


def striped(idx):
    return np.tile(idx.reshape(-1, 16).T, (8, 1)).astype(np.uint16)


def unstriped(offs):
    return offs[:16].T.reshape(-1).astype(np.int64)


def pack_weight(w):
    k, n = w.shape
    w = f64(np.asarray(w, np.float32).astype(ml_dtypes.bfloat16)).reshape(k // 32, 32, n)
    amax = np.abs(w).max(1)
    byte = np.clip(np.where(amax > 0, np.frexp(amax)[1] - 1 + 127 - 7, 1), 1, 254)
    scaled = (w * np.exp2(127.0 - byte)[:, None, :]).reshape(k, n).astype(np.float32)
    words = np.ascontiguousarray(scaled.reshape(k // 512, 128, 4, n).transpose(0, 1, 3, 2)).astype(ml_dtypes.float8_e4m3fn).view(np.uint8)
    return words, np.ascontiguousarray(byte.astype(np.uint8).reshape(k // 512, 16, n))


def unpack_weight(words, scales):
    g, p, n, _ = words.shape
    vals = np.ascontiguousarray(words).view(ml_dtypes.float8_e4m3fn).astype(np.float64) * np.repeat(np.exp2(scales.astype(np.float64) - 127.0), 8, axis=1)[..., None]
    return vals.transpose(0, 1, 3, 2).reshape(g * 512, n)


def relu(v):
    return np.maximum(v, 0.0)


K, T, S, H, N, U = 1024, 2048, 1024, 512, 256, 1024


def setup_inputs():
    n = np.random.standard_normal
    s = mx_kscale(K)[:, None]
    u = mx_kscale(H)
    packed_xT = pack_weight(n((K, T)) * s)
    return {
        "x_words": packed_xT[0],
        "x_scales": packed_xT[1],
        "w1": (n((K, H)) / np.sqrt(2 * K) / s * u).astype(np.float32),
        "w2": (n((K, H)) / np.sqrt(2 * K) / s * u).astype(np.float32),
        "w3": (n((H, N)) / np.sqrt(H) / u[:, None]).astype(np.float32),
        "offs": striped(np.random.permutation(T)[:S]),
        "src": striped(np.random.permutation(S)[(S * np.random.uniform(0, 1, U) ** 4).astype(np.int64)]),
        "dst": striped(np.random.permutation(S)),
    }


def reference(x_words, x_scales, w1, w2, w3, offs, src, dst):
    xq = unpack_weight(x_words, x_scales)[:, unstriped(offs)]
    y = mxq(f64(w1), 0, "e4m3").T @ xq
    e = mxq(f64(w2), 0, "e4m3").T @ xq
    z = relu(y[:, unstriped(src)] + e[:, unstriped(dst)])
    return mxq(f64(w3), 0, "e4m3").T @ mxq(z, 0, "e4m3")

@@ -1,0 +1,227 @@
+from contextlib import ExitStack
+
+import concourse.mybir as mybir
+
+K, T, S, H, N = 1024, 2048, 1024, 512, 256
+FLOPS = 2 * (2 * K * H * S + H * N * S)
+
+F32 = mybir.dt.float32
+BF16 = mybir.dt.bfloat16
+I32 = mybir.dt.int32
+U32 = mybir.dt.uint32
+U16 = mybir.dt.uint16
+U8 = mybir.dt.uint8
+FP8X4 = mybir.dt.float8_e4m3fn_x4
+ACT = mybir.ActivationFunctionType
+ADD = mybir.AluOpType.add
+
+P = 128
+PACK = 4
+PASSES = K // (P * PACK)
+HALF = 512
+EDGE_CHUNKS = (256, 256, 256, 128, 128)
+
+
+def tile_picked_hub_relu_p_kernel(
+    tc, x_words, x_scales, w1, w2, w3, offs, src, dst, out
+):
+    nc = tc.nc
+    with ExitStack() as ctx:
+        lists = ctx.enter_context(tc.tile_pool(name="lists", bufs=1))
+        keep = ctx.enter_context(tc.tile_pool(name="keep", bufs=1))
+        acc = ctx.enter_context(tc.psum_pool(name="acc", bufs=6))
+        fin = ctx.enter_context(tc.psum_pool(name="fin", bufs=2))
+
+        def sb(shape, dtype, name, tag=None):
+            return keep.tile(shape, dtype, name=name, tag=tag or name, align_bytes=64)
+
+        offs_sb = lists.tile([P, S // 16], U16, name="offs_sb")
+        src_sb = lists.tile([P, S // 16], U16, name="src_sb")
+        dst_sb = lists.tile([P, S // 16], U16, name="dst_sb")
+
+        x_scale_table = sb([P, T], U8, "x_scale_table")
+        nc.vector.memset(x_scale_table[:].bitcast(I32), 0)
+        nc.sync.dma_start(offs_sb[:], offs)
+        nc.sync.dma_start(src_sb[:], src)
+        nc.sync.dma_start(dst_sb[:], dst)
+        x_word_table = [sb([P, T], U32, f"x_word_table{z}") for z in range(PASSES)]
+        for z, cuts in enumerate(((0, 1024, 2048), (0, 768, 1536, 2048))):
+            words = x_words[z].rearrange("p c r -> p (c r)").bitcast(I32)
+            for c0, c1 in zip(cuts, cuts[1:]):
+                nc.sync.dma_start(out=x_word_table[z][:, c0:c1].bitcast(I32), in_=words[:, c0:c1])
+        for q in range(4):
+            nc.sync.dma_start(
+                out=x_scale_table[32 * q : 32 * q + 4 * PASSES, :].bitcast(I32),
+                in_=x_scales[:, 4 * q : 4 * q + 4, :].bitcast(I32),
+            )
+
+        def load_pass(w, z, name):
+            raw = sb([P, PACK, H], F32, name)
+            nc.sync.dma_start(
+                out=raw[:], in_=w[512 * z : 512 * (z + 1), :].rearrange("(p j) c -> p j c", j=PACK)
+            )
+            return raw
+
+        w1_raw = [load_pass(w1, z, f"w1_raw{z}") for z in range(PASSES)]
+        w2_raw = [load_pass(w2, z, f"w2_raw{z}") for z in range(PASSES)]
+        w3_raw = sb([P, PACK, N], F32, "w3_raw")
+        w3_rows = w3.rearrange("(b t r) n -> t b r n", t=PACK, r=8)
+        for t in range(PACK):
+            nc.sync.dma_start(out=w3_raw[:, t, :], in_=w3_rows[t])
+
+        x_codes = [sb([P, S], U32, f"x_codes{z}") for z in range(PASSES)]
+        for z in range(PASSES):
+            nc.vector.tensor_copy(x_codes[z][:], x_word_table[z][:].indirect(offs_sb[:]))
+        x_scale = []
+
+        def pick_scales(h, tag):
+            x_scale.append(sb([P, HALF], U8, f"x_scale{h}", tag))
+            nc.vector.tensor_copy(
+                x_scale[h][:], x_scale_table[:].indirect(offs_sb[:, h * HALF // 16 : (h + 1) * HALF // 16])
+            )
+
+        def deal(copy, rounded, raw, t):
+            copy(
+                rounded.rearrange("p (b h r j) -> p b h j r", h=2, r=4, j=PACK),
+                raw[:].rearrange("p j (b t h r) -> p t b h j r", t=PACK, h=2, r=4)[:, t],
+            )
+
+        def deal_act(rounded, raw, t):
+            nc.scalar.activation(
+                rounded.rearrange("p (b r j) -> p b j r", r=8, j=PACK),
+                raw[:].rearrange("p j (b t r) -> p t b j r", t=PACK, r=8)[:, t],
+                ACT.Copy,
+            )
+
+        def quantize(rounded, name):
+            width = rounded.shape[1] // PACK
+            codes = sb([P, width], U32, name + "_codes")
+            scales = sb([P, width], U8, name + "_scales")
+            nc.vector.quantize_mx(out=codes[:].bitcast(FP8X4), scales=scales[:], in_=rounded[:])
+            return codes, scales
+
+        def piece(pair, i):
+            return pair[0][:, i * P : (i + 1) * P], pair[1][:, i * P : (i + 1) * P]
+
+        def product_pass(bank, weights, z, h):
+            cols = slice(h * HALF, (h + 1) * HALF)
+            nc.tensor.matmul_mx(
+                out=bank[:],
+                lhsT=weights[0].bitcast(FP8X4),
+                lhsT_scale=weights[1],
+                rhs=x_codes[z][:, cols].bitcast(FP8X4),
+                rhs_scale=x_scale[h][4 * z : P, :],
+                start=(z == 0),
+                stop=(z == PASSES - 1),
+            )
+
+        w1_mx = {}
+        pick_scales(0, None)
+        first = sb([P, H], BF16, "w1_first")
+        deal_act(first[:], w1_raw[0], 0)
+        w1_mx[0, 0] = piece(quantize(first, "w1_first"), 0)
+        pick_scales(1, "w1_first")
+        both = {t: sb([P, PASSES * H], BF16, f"w1_rounded{t}") for t in range(1, PACK)}
+        for t in range(1, PACK):
+            deal(nc.scalar.copy, both[t][:, 0:H], w1_raw[0], t)
+        second = sb([P, H], BF16, "w1_second")
+        deal(nc.scalar.copy, second[:], w1_raw[1], 0)
+        w1_mx[1, 0] = piece(quantize(second, "w1_second"), 0)
+        for t in range(1, PACK):
+            deal(nc.vector.tensor_copy if t == 3 else nc.scalar.copy, both[t][:, H : 2 * H], w1_raw[1], t)
+            both_mx = quantize(both[t], f"w1_{t}")
+            for z in range(PASSES):
+                w1_mx[z, t] = piece(both_mx, z)
+
+        y = [sb([P, S], F32, f"y{t}") for t in range(PACK)]
+        for t in range(PACK):
+            banks = [acc.tile([P, HALF], F32, name="bank") for h in range(2)]
+            for z in range(PASSES):
+                for h in range(2):
+                    product_pass(banks[h], w1_mx[z, t], z, h)
+            for h in range(2):
+                copy = nc.vector.tensor_copy if (t, h) == (0, 1) else nc.scalar.copy
+                copy(y[t][:, h * HALF : (h + 1) * HALF], banks[h][:])
+
+        y_picked = {}
+
+        def pick_y(t, h, tag):
+            y_picked[t, h] = sb([P, HALF], F32, f"y_picked{t}{h}", tag)
+            nc.vector.tensor_copy(
+                y_picked[t, h][:], y[t][:].indirect(src_sb[:, h * HALF // 16 : (h + 1) * HALF // 16])
+            )
+
+        for t in range(2):
+            for h in range(2):
+                pick_y(t, h, None)
+
+        w2_mx = []
+        for t in range(PACK):
+            rounded = sb([P, PASSES * H], BF16, f"w2_rounded{t}")
+            for z in range(PASSES):
+                deal(nc.scalar.copy, rounded[:, z * H : (z + 1) * H], w2_raw[z], t)
+            w2_mx.append(quantize(rounded, f"w2_{t}"))
+            pick_y(2 + t // 2, t % 2, f"w2_rounded{t}")
+
+        e = [sb([P, S], F32, f"e{t}") for t in range(PACK)]
+        for t in range(PACK):
+            for h in range(2):
+                bank = acc.tile([P, HALF], F32, name="bank")
+                for z in range(PASSES):
+                    product_pass(bank, piece(w2_mx[t], z), z, h)
+                nc.scalar.copy(e[t][:, h * HALF : (h + 1) * HALF], bank[:])
+
+        w3_rounded = sb([P, PACK * N], BF16, "w3_rounded")
+        nc.scalar.copy(
+            w3_rounded[:].rearrange("p (c i j) -> p c j i", i=4, j=PACK),
+            w3_raw[:].rearrange("p j (c i) -> p c j i", i=4),
+        )
+        w3_mx = quantize(w3_rounded, "w3")
+
+        out_rows = out.rearrange("(m p) r -> p m r", p=P)
+        starts = [sum(EDGE_CHUNKS[:c]) for c in range(len(EDGE_CHUNKS))]
+
+        def add_targets(c):
+            r0, n = starts[c], EDGE_CHUNKS[c]
+            sums = sb([P, PACK, n], F32, f"sums{c}", f"z{c - 2}" if c >= 2 else None)
+            for t in range(PACK):
+                h, a = divmod(r0, HALF)
+                nc.vector.tensor_tensor(
+                    sums[:, t, :],
+                    e[t][:].indirect(dst_sb[:, r0 // 16 : (r0 + n) // 16]),
+                    y_picked[t, h][:, a : a + n],
+                    ADD,
+                )
+            z_rounded = sb([P, PACK * n], BF16, f"z{c}")
+            nc.scalar.activation(
+                z_rounded[:].rearrange("p (c i j) -> p c j i", i=4, j=PACK),
+                sums[:].rearrange("p j (c i) -> p c j i", i=4),
+                ACT.Relu,
+            )
+            return z_rounded
+
+        def finish(c, z_rounded):
+            r0, n = starts[c], EDGE_CHUNKS[c]
+            z_codes, z_scales = quantize(z_rounded, f"z{c}")
+            bank = fin.tile([P, 2, n], F32, name="out_bank")
+            for m in range(N // P):
+                codes, scales = piece(w3_mx, m)
+                nc.tensor.matmul_mx(
+                    out=bank[:, m, :],
+                    lhsT=codes.bitcast(FP8X4),
+                    lhsT_scale=scales,
+                    rhs=z_codes[:].bitcast(FP8X4),
+                    rhs_scale=z_scales[:],
+                    start=True,
+                    stop=True,
+                )
+            result = sb([P, 2, n], F32, f"result{c}")
+            nc.scalar.copy(result[:], bank[:])
+            nc.sync.dma_start(out=out_rows[:, :, r0 : r0 + n], in_=result[:])
+
+        pending = add_targets(0)
+        for c in range(1, len(EDGE_CHUNKS)):
+            following = add_targets(c)
+            finish(c - 1, pending)
+            pending = following
+        finish(len(EDGE_CHUNKS) - 1, pending)

@@ -45,40 +45,45 @@ def tile_picked_hub_relu_p_kernel(
         nc.sync.dma_start(src_sb[:], src)
         nc.sync.dma_start(dst_sb[:], dst)
         x_word_table = [sb([P, T], U32, f"x_word_table{z}") for z in range(PASSES)]
-        for z, cuts in enumerate(((0, 1024, 2048), (0, 768, 1536, 2048))):
+
+        def load_words(z, c0, c1):
             words = x_words[z].rearrange("p c r -> p (c r)").bitcast(I32)
-            for c0, c1 in zip(cuts, cuts[1:]):
-                nc.sync.dma_start(out=x_word_table[z][:, c0:c1].bitcast(I32), in_=words[:, c0:c1])
+            nc.sync.dma_start(out=x_word_table[z][:, c0:c1].bitcast(I32), in_=words[:, c0:c1])
+
+        def load_pass(w, z, name, cuts=(0, PACK)):
+            raw = sb([P, PACK, H], F32, name)
+            rows = w[512 * z : 512 * (z + 1), :].rearrange("(p j) c -> p j c", j=PACK)
+            for j0, j1 in zip(cuts, cuts[1:]):
+                nc.sync.dma_start(out=raw[:, j0:j1, :], in_=rows[:, j0:j1, :])
+            return raw
+
+        for c0 in range(0, T, T // 4):
+            load_words(0, c0, c0 + T // 4)
+        w1_raw = [load_pass(w1, 0, "w1_raw0")]
         for q in range(4):
             nc.sync.dma_start(
                 out=x_scale_table[32 * q : 32 * q + 4 * PASSES, :].bitcast(I32),
                 in_=x_scales[:, 4 * q : 4 * q + 4, :].bitcast(I32),
             )
-
-        def load_pass(w, z, name):
-            raw = sb([P, PACK, H], F32, name)
-            nc.sync.dma_start(
-                out=raw[:], in_=w[512 * z : 512 * (z + 1), :].rearrange("(p j) c -> p j c", j=PACK)
-            )
-            return raw
-
-        w1_raw = [load_pass(w1, z, f"w1_raw{z}") for z in range(PASSES)]
+        load_words(1, 0, T)
+        w1_raw.append(load_pass(w1, 1, "w1_raw1"))
         w2_raw = [load_pass(w2, z, f"w2_raw{z}") for z in range(PASSES)]
         w3_raw = sb([P, PACK, N], F32, "w3_raw")
         w3_rows = w3.rearrange("(b t r) n -> t b r n", t=PACK, r=8)
         for t in range(PACK):
             nc.sync.dma_start(out=w3_raw[:, t, :], in_=w3_rows[t])
 
-        x_codes = [sb([P, S], U32, f"x_codes{z}") for z in range(PASSES)]
-        for z in range(PASSES):
-            nc.vector.tensor_copy(x_codes[z][:], x_word_table[z][:].indirect(offs_sb[:]))
-        x_scale = []
+        x_codes = {}
 
-        def pick_scales(h, tag):
-            x_scale.append(sb([P, HALF], U8, f"x_scale{h}", tag))
+        def pick_words(z, c0, n, tag):
+            x_codes[z, c0] = sb([P, n], U32, f"x_codes{z}_{c0}", tag)
             nc.vector.tensor_copy(
-                x_scale[h][:], x_scale_table[:].indirect(offs_sb[:, h * HALF // 16 : (h + 1) * HALF // 16])
+                x_codes[z, c0][:], x_word_table[z][:].indirect(offs_sb[:, c0 // 16 : (c0 + n) // 16])
             )
+
+        pick_words(0, 0, S, None)
+        x_scale = sb([P, S], U8, "x_scale")
+        nc.vector.tensor_copy(x_scale[:], x_scale_table[:].indirect(offs_sb[:]))
 
         def deal(copy, rounded, raw, t):
             copy(
@@ -103,45 +108,49 @@ def tile_picked_hub_relu_p_kernel(
         def piece(pair, i):
             return pair[0][:, i * P : (i + 1) * P], pair[1][:, i * P : (i + 1) * P]
 
-        def product_pass(bank, weights, z, h):
-            cols = slice(h * HALF, (h + 1) * HALF)
+        def multiply(bank, weights, z, c0, n, stop):
+            base = 768 if (z, c0) == (1, 768) else 0
             nc.tensor.matmul_mx(
-                out=bank[:],
+                out=bank[:, c0 % HALF : c0 % HALF + n],
                 lhsT=weights[0].bitcast(FP8X4),
                 lhsT_scale=weights[1],
-                rhs=x_codes[z][:, cols].bitcast(FP8X4),
-                rhs_scale=x_scale[h][4 * z : P, :],
+                rhs=x_codes[z, base][:, c0 - base : c0 - base + n].bitcast(FP8X4),
+                rhs_scale=x_scale[4 * z : P, c0 : c0 + n],
                 start=(z == 0),
-                stop=(z == PASSES - 1),
+                stop=stop,
             )
 
-        w1_mx = {}
-        pick_scales(0, None)
-        first = sb([P, H], BF16, "w1_first")
-        deal_act(first[:], w1_raw[0], 0)
-        w1_mx[0, 0] = piece(quantize(first, "w1_first"), 0)
-        pick_scales(1, "w1_first")
-        both = {t: sb([P, PASSES * H], BF16, f"w1_rounded{t}") for t in range(1, PACK)}
+        def open_plane(weights):
+            banks = [acc.tile([P, HALF], F32, name="bank") for h in range(2)]
+            for h in range(2):
+                multiply(banks[h], weights, 0, h * HALF, HALF, False)
+            return banks
+
+        def close_plane(banks, weights, target):
+            multiply(banks[0], weights, 1, 0, HALF, True)
+            nc.scalar.copy(target[:, 0:HALF], banks[0][:])
+            multiply(banks[1], weights, 1, 512, 256, False)
+            multiply(banks[1], weights, 1, 768, 256, True)
+            nc.scalar.copy(target[:, HALF:S], banks[1][:])
+
+        first = sb([P, PACK * H], BF16, "w1_first")
+        deal_act(first[:, 0:H], w1_raw[0], 0)
         for t in range(1, PACK):
-            deal(nc.scalar.copy, both[t][:, 0:H], w1_raw[0], t)
-        second = sb([P, H], BF16, "w1_second")
-        deal(nc.scalar.copy, second[:], w1_raw[1], 0)
-        w1_mx[1, 0] = piece(quantize(second, "w1_second"), 0)
-        for t in range(1, PACK):
-            deal(nc.vector.tensor_copy if t == 3 else nc.scalar.copy, both[t][:, H : 2 * H], w1_raw[1], t)
-            both_mx = quantize(both[t], f"w1_{t}")
-            for z in range(PASSES):
-                w1_mx[z, t] = piece(both_mx, z)
+            deal(nc.scalar.copy, first[:, t * H : (t + 1) * H], w1_raw[0], t)
+        first_mx = quantize(first, "w1_first")
+        opened = [open_plane(piece(first_mx, t)) for t in range(3)]
+        pick_words(1, 0, 768, "w1_first")
+        second_mx = []
+        for t in range(PACK):
+            second = sb([P, H], BF16, f"w1_second{t}", "w1_second1" if t == 3 else None)
+            deal(nc.vector.tensor_copy if t == 3 else nc.scalar.copy, second[:], w1_raw[1], t)
+            second_mx.append(piece(quantize(second, f"w1_second{t}"), 0))
+            if t == 0:
+                pick_words(1, 768, 256, "w1_second0")
 
         y = [sb([P, S], F32, f"y{t}") for t in range(PACK)]
         for t in range(PACK):
-            banks = [acc.tile([P, HALF], F32, name="bank") for h in range(2)]
-            for z in range(PASSES):
-                for h in range(2):
-                    product_pass(banks[h], w1_mx[z, t], z, h)
-            for h in range(2):
-                copy = nc.vector.tensor_copy if (t, h) == (0, 1) else nc.scalar.copy
-                copy(y[t][:, h * HALF : (h + 1) * HALF], banks[h][:])
+            close_plane(opened[t] if t < 3 else open_plane(piece(first_mx, t)), second_mx[t], y[t])
 
         y_picked = {}
 
@@ -158,51 +167,61 @@ def tile_picked_hub_relu_p_kernel(
         w2_mx = []
         for t in range(PACK):
             rounded = sb([P, PASSES * H], BF16, f"w2_rounded{t}")
-            for z in range(PASSES):
-                deal(nc.scalar.copy, rounded[:, z * H : (z + 1) * H], w2_raw[z], t)
+            nc.gpsimd.tensor_scalar(
+                rounded[:, 0:H].rearrange("p (b r j) -> p b r j", r=8, j=PACK),
+                w2_raw[0][:].rearrange("p j (b t r) -> p t b r j", t=PACK, r=8)[:, t],
+                1.0,
+                0.0,
+                mybir.AluOpType.mult,
+                ADD,
+            )
+            deal(nc.scalar.copy, rounded[:, H : 2 * H], w2_raw[1], t)
             w2_mx.append(quantize(rounded, f"w2_{t}"))
             pick_y(2 + t // 2, t % 2, f"w2_rounded{t}")
 
         e = [sb([P, S], F32, f"e{t}") for t in range(PACK)]
         for t in range(PACK):
-            for h in range(2):
-                bank = acc.tile([P, HALF], F32, name="bank")
-                for z in range(PASSES):
-                    product_pass(bank, piece(w2_mx[t], z), z, h)
-                nc.scalar.copy(e[t][:, h * HALF : (h + 1) * HALF], bank[:])
+            close_plane(open_plane(piece(w2_mx[t], 0)), piece(w2_mx[t], 1), e[t])
 
         w3_rounded = sb([P, PACK * N], BF16, "w3_rounded")
-        nc.scalar.copy(
-            w3_rounded[:].rearrange("p (c i j) -> p c j i", i=4, j=PACK),
-            w3_raw[:].rearrange("p j (c i) -> p c j i", i=4),
+        nc.gpsimd.tensor_scalar(
+            w3_rounded[:].rearrange("p (c j) -> p c j", j=PACK),
+            w3_raw[:].rearrange("p j c -> p c j"),
+            1.0,
+            0.0,
+            mybir.AluOpType.mult,
+            ADD,
         )
         w3_mx = quantize(w3_rounded, "w3")
 
         out_rows = out.rearrange("(m p) r -> p m r", p=P)
-        starts = [sum(EDGE_CHUNKS[:c]) for c in range(len(EDGE_CHUNKS))]
 
-        def add_targets(c):
-            r0, n = starts[c], EDGE_CHUNKS[c]
-            sums = sb([P, PACK, n], F32, f"sums{c}", f"z{c - 2}" if c >= 2 else None)
+        def add_targets(r0, n, tag):
+            sums = sb([P, PACK, n], F32, f"sums{r0}", tag)
+            h, a = divmod(r0, HALF)
             for t in range(PACK):
-                h, a = divmod(r0, HALF)
-                nc.vector.tensor_tensor(
-                    sums[:, t, :],
-                    e[t][:].indirect(dst_sb[:, r0 // 16 : (r0 + n) // 16]),
-                    y_picked[t, h][:, a : a + n],
-                    ADD,
-                )
-            z_rounded = sb([P, PACK * n], BF16, f"z{c}")
+                step = min(n, 256) if t == PACK - 1 else n
+                for c in range(0, n, step):
+                    nc.vector.tensor_tensor(
+                        sums[:, t, c : c + step],
+                        e[t][:].indirect(dst_sb[:, (r0 + c) // 16 : (r0 + c + step) // 16]),
+                        y_picked[t, h][:, a + c : a + c + step],
+                        ADD,
+                    )
+            return sums
+
+        def rectify(r0, sums):
+            z_rounded = sb([P, PACK * sums.shape[2]], BF16, f"z{r0}")
             nc.scalar.activation(
                 z_rounded[:].rearrange("p (c i j) -> p c j i", i=4, j=PACK),
-                sums[:].rearrange("p j (c i) -> p c j i", i=4),
+                sums.rearrange("p j (c i) -> p c j i", i=4),
                 ACT.Relu,
             )
             return z_rounded
 
-        def finish(c, z_rounded):
-            r0, n = starts[c], EDGE_CHUNKS[c]
-            z_codes, z_scales = quantize(z_rounded, f"z{c}")
+        def finish(r0, z_rounded):
+            n = z_rounded.shape[1] // PACK
+            z_codes, z_scales = quantize(z_rounded, f"z{r0}")
             bank = fin.tile([P, 2, n], F32, name="out_bank")
             for m in range(N // P):
                 codes, scales = piece(w3_mx, m)
@@ -215,13 +234,18 @@ def tile_picked_hub_relu_p_kernel(
                     start=True,
                     stop=True,
                 )
-            result = sb([P, 2, n], F32, f"result{c}")
+            result = sb([P, 2, n], F32, f"result{r0}")
             nc.scalar.copy(result[:], bank[:])
             nc.sync.dma_start(out=out_rows[:, :, r0 : r0 + n], in_=result[:])
 
-        pending = add_targets(0)
-        for c in range(1, len(EDGE_CHUNKS)):
-            following = add_targets(c)
-            finish(c - 1, pending)
-            pending = following
-        finish(len(EDGE_CHUNKS) - 1, pending)
+        sums = add_targets(0, 512, None)
+        z0 = rectify(0, sums[:, :, 0:256])
+        z256 = rectify(256, sums[:, :, 256:512])
+        z512 = rectify(512, add_targets(512, 256, None)[:])
+        finish(0, z0)
+        finish(256, z256)
+        z768 = rectify(768, add_targets(768, 128, "z256")[:])
+        finish(512, z512)
+        z896 = rectify(896, add_targets(896, 128, "z512")[:])
+        finish(768, z768)
+        finish(896, z896)

@@ -29,11 +29,11 @@ def tile_picked_hub_relu_p_kernel(
     with ExitStack() as ctx:
         lists = ctx.enter_context(tc.tile_pool(name="lists", bufs=1))
         keep = ctx.enter_context(tc.tile_pool(name="keep", bufs=1))
-        acc = ctx.enter_context(tc.psum_pool(name="acc", bufs=6))
-        fin = ctx.enter_context(tc.psum_pool(name="fin", bufs=2))
+        acc = ctx.enter_context(tc.psum_pool(name="acc", bufs=4))
+        fin = ctx.enter_context(tc.psum_pool(name="fin", bufs=4))
 
-        def sb(shape, dtype, name, tag=None):
-            return keep.tile(shape, dtype, name=name, tag=tag or name, align_bytes=64)
+        def sb(shape, dtype, name, tag=None, bufs=1):
+            return keep.tile(shape, dtype, name=name, tag=tag or name, bufs=bufs, align_bytes=64)
 
         offs_sb = lists.tile([P, S // 16], U16, name="offs_sb")
         src_sb = lists.tile([P, S // 16], U16, name="src_sb")
@@ -73,20 +73,18 @@ def tile_picked_hub_relu_p_kernel(
         for t in range(PACK):
             nc.sync.dma_start(out=w3_raw[:, t, :], in_=w3_rows[t])
 
-        x_codes = {}
+        x_codes = []
 
-        def pick_words(z, c0, n, tag):
-            x_codes[z, c0] = sb([P, n], U32, f"x_codes{z}_{c0}", tag)
-            nc.vector.tensor_copy(
-                x_codes[z, c0][:], x_word_table[z][:].indirect(offs_sb[:, c0 // 16 : (c0 + n) // 16])
-            )
+        def pick_words(z, tag):
+            x_codes.append(sb([P, S], U32, f"x_codes{z}", tag))
+            nc.vector.tensor_copy(x_codes[z][:], x_word_table[z][:].indirect(offs_sb[:]))
 
-        pick_words(0, 0, S, None)
+        pick_words(0, None)
         x_scale = sb([P, S], U8, "x_scale")
         nc.vector.tensor_copy(x_scale[:], x_scale_table[:].indirect(offs_sb[:]))
 
-        def deal(copy, rounded, raw, t):
-            copy(
+        def deal_scalar(rounded, raw, t):
+            nc.scalar.copy(
                 rounded.rearrange("p (b h r j) -> p b h j r", h=2, r=4, j=PACK),
                 raw[:].rearrange("p j (b t h r) -> p t b h j r", t=PACK, h=2, r=4)[:, t],
             )
@@ -96,6 +94,16 @@ def tile_picked_hub_relu_p_kernel(
                 rounded.rearrange("p (b r j) -> p b j r", r=8, j=PACK),
                 raw[:].rearrange("p j (b t r) -> p t b j r", t=PACK, r=8)[:, t],
                 ACT.Copy,
+            )
+
+        def deal_gpsimd(rounded, raw, t):
+            nc.gpsimd.tensor_scalar(
+                rounded.rearrange("p (b r j) -> p b r j", r=8, j=PACK),
+                raw[:].rearrange("p j (b t r) -> p t b r j", t=PACK, r=8)[:, t],
+                1.0,
+                0.0,
+                mybir.AluOpType.mult,
+                ADD,
             )
 
         def quantize(rounded, name):
@@ -108,80 +116,68 @@ def tile_picked_hub_relu_p_kernel(
         def piece(pair, i):
             return pair[0][:, i * P : (i + 1) * P], pair[1][:, i * P : (i + 1) * P]
 
-        def multiply(bank, weights, z, c0, n, stop):
-            base = 768 if (z, c0) == (1, 768) else 0
+        def multiply(bank, weights, z, h):
+            cols = slice(h * HALF, (h + 1) * HALF)
             nc.tensor.matmul_mx(
-                out=bank[:, c0 % HALF : c0 % HALF + n],
+                out=bank[:],
                 lhsT=weights[0].bitcast(FP8X4),
                 lhsT_scale=weights[1],
-                rhs=x_codes[z, base][:, c0 - base : c0 - base + n].bitcast(FP8X4),
-                rhs_scale=x_scale[4 * z : P, c0 : c0 + n],
+                rhs=x_codes[z][:, cols].bitcast(FP8X4),
+                rhs_scale=x_scale[4 * z : P, cols],
                 start=(z == 0),
-                stop=stop,
+                stop=(z == PASSES - 1),
             )
 
-        def open_plane(weights):
+        def plane(weights, target, copies=(nc.scalar.copy, nc.scalar.copy)):
             banks = [acc.tile([P, HALF], F32, name="bank") for h in range(2)]
+            for z in range(PASSES):
+                for h in range(2):
+                    multiply(banks[h], weights[z], z, h)
             for h in range(2):
-                multiply(banks[h], weights, 0, h * HALF, HALF, False)
-            return banks
-
-        def close_plane(banks, weights, target):
-            multiply(banks[0], weights, 1, 0, HALF, True)
-            nc.scalar.copy(target[:, 0:HALF], banks[0][:])
-            multiply(banks[1], weights, 1, 512, 256, False)
-            multiply(banks[1], weights, 1, 768, 256, True)
-            nc.scalar.copy(target[:, HALF:S], banks[1][:])
+                copies[h](target[:, h * HALF : (h + 1) * HALF], banks[h][:])
 
         first = sb([P, PACK * H], BF16, "w1_first")
         deal_act(first[:, 0:H], w1_raw[0], 0)
         for t in range(1, PACK):
-            deal(nc.scalar.copy, first[:, t * H : (t + 1) * H], w1_raw[0], t)
+            deal_scalar(first[:, t * H : (t + 1) * H], w1_raw[0], t)
         first_mx = quantize(first, "w1_first")
-        opened = [open_plane(piece(first_mx, t)) for t in range(3)]
-        pick_words(1, 0, 768, "w1_first")
-        second_mx = []
+        pick_words(1, "w1_raw0")
+        w1_mx = []
         for t in range(PACK):
-            second = sb([P, H], BF16, f"w1_second{t}", "w1_second1" if t == 3 else None)
-            deal(nc.vector.tensor_copy if t == 3 else nc.scalar.copy, second[:], w1_raw[1], t)
-            second_mx.append(piece(quantize(second, f"w1_second{t}"), 0))
-            if t == 0:
-                pick_words(1, 768, 256, "w1_second0")
+            second = sb([P, H], BF16, f"w1_second{t}")
+            (deal_gpsimd if t == PACK - 1 else deal_scalar)(second[:], w1_raw[1], t)
+            w1_mx.append((piece(first_mx, t), piece(quantize(second, f"w1_second{t}"), 0)))
 
         y = [sb([P, S], F32, f"y{t}") for t in range(PACK)]
-        for t in range(PACK):
-            close_plane(opened[t] if t < 3 else open_plane(piece(first_mx, t)), second_mx[t], y[t])
+        plane(w1_mx[0], y[0], (nc.scalar.copy, nc.vector.tensor_copy))
+        for t in (1, 2):
+            plane(w1_mx[t], y[t])
 
         y_picked = {}
 
-        def pick_y(t, h, tag):
-            y_picked[t, h] = sb([P, HALF], F32, f"y_picked{t}{h}", tag)
-            nc.vector.tensor_copy(
-                y_picked[t, h][:], y[t][:].indirect(src_sb[:, h * HALF // 16 : (h + 1) * HALF // 16])
-            )
+        def pick_y(planes, tag):
+            picked = sb([P, len(planes), S], F32, f"y_picked{planes[0]}", tag)
+            for i, t in enumerate(planes):
+                y_picked[t] = picked[:, i, :]
+                for h in range(2):
+                    nc.vector.tensor_copy(
+                        picked[:, i, h * HALF : (h + 1) * HALF],
+                        y[t][:].indirect(src_sb[:, h * HALF // 16 : (h + 1) * HALF // 16]),
+                    )
 
-        for t in range(2):
-            for h in range(2):
-                pick_y(t, h, None)
-
+        pick_y((0, 1), None)
         w2_mx = []
         for t in range(PACK):
             rounded = sb([P, PASSES * H], BF16, f"w2_rounded{t}")
-            nc.gpsimd.tensor_scalar(
-                rounded[:, 0:H].rearrange("p (b r j) -> p b r j", r=8, j=PACK),
-                w2_raw[0][:].rearrange("p j (b t r) -> p t b r j", t=PACK, r=8)[:, t],
-                1.0,
-                0.0,
-                mybir.AluOpType.mult,
-                ADD,
-            )
-            deal(nc.scalar.copy, rounded[:, H : 2 * H], w2_raw[1], t)
+            deal_gpsimd(rounded[:, 0:H], w2_raw[0], t)
+            deal_scalar(rounded[:, H : 2 * H], w2_raw[1], t)
             w2_mx.append(quantize(rounded, f"w2_{t}"))
-            pick_y(2 + t // 2, t % 2, f"w2_rounded{t}")
+        plane(w1_mx[3], y[3])
+        pick_y((2, 3), "w2_raw1")
 
         e = [sb([P, S], F32, f"e{t}") for t in range(PACK)]
         for t in range(PACK):
-            close_plane(open_plane(piece(w2_mx[t], 0)), piece(w2_mx[t], 1), e[t])
+            plane([piece(w2_mx[t], z) for z in range(PASSES)], e[t])
 
         w3_rounded = sb([P, PACK * N], BF16, "w3_rounded")
         nc.gpsimd.tensor_scalar(
@@ -196,25 +192,19 @@ def tile_picked_hub_relu_p_kernel(
 
         out_rows = out.rearrange("(m p) r -> p m r", p=P)
 
-        def add_targets(r0, n, tag):
-            sums = sb([P, PACK, n], F32, f"sums{r0}", tag)
-            h, a = divmod(r0, HALF)
+        def edge_values(r0, n):
+            sums = sb([P, PACK, n], F32, f"sums{r0}", "sums", 2)
             for t in range(PACK):
-                step = min(n, 256) if t == PACK - 1 else n
-                for c in range(0, n, step):
-                    nc.vector.tensor_tensor(
-                        sums[:, t, c : c + step],
-                        e[t][:].indirect(dst_sb[:, (r0 + c) // 16 : (r0 + c + step) // 16]),
-                        y_picked[t, h][:, a + c : a + c + step],
-                        ADD,
-                    )
-            return sums
-
-        def rectify(r0, sums):
-            z_rounded = sb([P, PACK * sums.shape[2]], BF16, f"z{r0}")
+                nc.vector.tensor_tensor(
+                    sums[:, t, :],
+                    e[t][:].indirect(dst_sb[:, r0 // 16 : (r0 + n) // 16]),
+                    y_picked[t][:, r0 : r0 + n],
+                    ADD,
+                )
+            z_rounded = sb([P, PACK * n], BF16, f"z{r0}")
             nc.scalar.activation(
                 z_rounded[:].rearrange("p (c i j) -> p c j i", i=4, j=PACK),
-                sums.rearrange("p j (c i) -> p c j i", i=4),
+                sums[:].rearrange("p j (c i) -> p c j i", i=4),
                 ACT.Relu,
             )
             return z_rounded
@@ -238,14 +228,10 @@ def tile_picked_hub_relu_p_kernel(
             nc.scalar.copy(result[:], bank[:])
             nc.sync.dma_start(out=out_rows[:, :, r0 : r0 + n], in_=result[:])
 
-        sums = add_targets(0, 512, None)
-        z0 = rectify(0, sums[:, :, 0:256])
-        z256 = rectify(256, sums[:, :, 256:512])
-        z512 = rectify(512, add_targets(512, 256, None)[:])
-        finish(0, z0)
-        finish(256, z256)
-        z768 = rectify(768, add_targets(768, 128, "z256")[:])
-        finish(512, z512)
-        z896 = rectify(896, add_targets(896, 128, "z512")[:])
-        finish(768, z768)
-        finish(896, z896)
+        starts = [sum(EDGE_CHUNKS[:c]) for c in range(len(EDGE_CHUNKS))]
+        pending = edge_values(starts[0], EDGE_CHUNKS[0])
+        for c in range(1, len(EDGE_CHUNKS)):
+            following = edge_values(starts[c], EDGE_CHUNKS[c])
+            finish(starts[c - 1], pending)
+            pending = following
+        finish(starts[-1], pending)

@@ -29,11 +29,10 @@ def tile_picked_hub_relu_p_kernel(
     with ExitStack() as ctx:
         lists = ctx.enter_context(tc.tile_pool(name="lists", bufs=1))
         keep = ctx.enter_context(tc.tile_pool(name="keep", bufs=1))
-        acc = ctx.enter_context(tc.psum_pool(name="acc", bufs=4))
-        fin = ctx.enter_context(tc.psum_pool(name="fin", bufs=4))
+        psum = ctx.enter_context(tc.psum_pool(name="psum", bufs=8))
 
-        def sb(shape, dtype, name, tag=None, bufs=1):
-            return keep.tile(shape, dtype, name=name, tag=tag or name, bufs=bufs, align_bytes=64)
+        def sb(shape, dtype, name, tag=None):
+            return keep.tile(shape, dtype, name=name, tag=tag or name, align_bytes=64)
 
         offs_sb = lists.tile([P, S // 16], U16, name="offs_sb")
         src_sb = lists.tile([P, S // 16], U16, name="src_sb")
@@ -42,46 +41,48 @@ def tile_picked_hub_relu_p_kernel(
         x_scale_table = sb([P, T], U8, "x_scale_table")
         nc.vector.memset(x_scale_table[:].bitcast(I32), 0)
         nc.sync.dma_start(offs_sb[:], offs)
-        nc.sync.dma_start(src_sb[:], src)
-        nc.sync.dma_start(dst_sb[:], dst)
-        x_word_table = [sb([P, T], U32, f"x_word_table{z}") for z in range(PASSES)]
-
-        def load_words(z, c0, c1):
-            words = x_words[z].rearrange("p c r -> p (c r)").bitcast(I32)
-            nc.sync.dma_start(out=x_word_table[z][:, c0:c1].bitcast(I32), in_=words[:, c0:c1])
-
-        def load_pass(w, z, name, cuts=(0, PACK)):
-            raw = sb([P, PACK, H], F32, name)
-            rows = w[512 * z : 512 * (z + 1), :].rearrange("(p j) c -> p j c", j=PACK)
-            for j0, j1 in zip(cuts, cuts[1:]):
-                nc.sync.dma_start(out=raw[:, j0:j1, :], in_=rows[:, j0:j1, :])
-            return raw
-
-        for c0 in range(0, T, T // 4):
-            load_words(0, c0, c0 + T // 4)
-        w1_raw = [load_pass(w1, 0, "w1_raw0")]
+        x_scale_rows = sb([P, T], U8, "x_scale_rows")
         for q in range(4):
+            rows = slice(32 * q, 32 * q + 4 * PASSES)
             nc.sync.dma_start(
-                out=x_scale_table[32 * q : 32 * q + 4 * PASSES, :].bitcast(I32),
+                out=x_scale_rows[rows, :].bitcast(I32),
                 in_=x_scales[:, 4 * q : 4 * q + 4, :].bitcast(I32),
             )
-        load_words(1, 0, T)
-        w1_raw.append(load_pass(w1, 1, "w1_raw1"))
+            nc.vector.tensor_copy(x_scale_table[rows, :].bitcast(I32), x_scale_rows[rows, :].bitcast(I32))
+
+        def load_words(z):
+            table = sb([P, T], U32, f"x_word_table{z}")
+            words = x_words[z].rearrange("p c r -> p (c r)").bitcast(I32)
+            nc.sync.dma_start(out=table[:].bitcast(I32), in_=words)
+            return table
+
+        def load_pass(w, z, name):
+            raw = sb([P, PACK, H], F32, name)
+            rows = w[512 * z : 512 * (z + 1), :].rearrange("(p j) c -> p j c", j=PACK)
+            nc.sync.dma_start(out=raw[:], in_=rows)
+            return raw
+
+        x_word_table, w1_raw = [], []
+        for z in range(PASSES):
+            x_word_table.append(load_words(z))
+            w1_raw.append(load_pass(w1, z, f"w1_raw{z}"))
+        nc.sync.dma_start(src_sb[:], src)
+        nc.sync.dma_start(dst_sb[:], dst)
         w2_raw = [load_pass(w2, z, f"w2_raw{z}") for z in range(PASSES)]
         w3_raw = sb([P, PACK, N], F32, "w3_raw")
         w3_rows = w3.rearrange("(b t r) n -> t b r n", t=PACK, r=8)
         for t in range(PACK):
             nc.sync.dma_start(out=w3_raw[:, t, :], in_=w3_rows[t])
 
-        x_codes = []
-
-        def pick_words(z, tag):
-            x_codes.append(sb([P, S], U32, f"x_codes{z}", tag))
-            nc.vector.tensor_copy(x_codes[z][:], x_word_table[z][:].indirect(offs_sb[:]))
-
-        pick_words(0, None)
         x_scale = sb([P, S], U8, "x_scale")
         nc.vector.tensor_copy(x_scale[:], x_scale_table[:].indirect(offs_sb[:]))
+
+        def pick_words(z, c0, n, tag=None):
+            codes = sb([P, n], U32, f"x_codes{z}_{c0}", tag)
+            nc.vector.tensor_copy(codes[:], x_word_table[z][:].indirect(offs_sb[:, c0 // 16 : (c0 + n) // 16]))
+            return [codes[:, c : c + HALF] for c in range(0, n, HALF)]
+
+        x_codes = [pick_words(0, 0, S)]
 
         def deal_scalar(rounded, raw, t):
             nc.scalar.copy(
@@ -89,111 +90,121 @@ def tile_picked_hub_relu_p_kernel(
                 raw[:].rearrange("p j (b t h r) -> p t b h j r", t=PACK, h=2, r=4)[:, t],
             )
 
-        def deal_act(rounded, raw, t):
-            nc.scalar.activation(
-                rounded.rearrange("p (b r j) -> p b j r", r=8, j=PACK),
-                raw[:].rearrange("p j (b t r) -> p t b j r", t=PACK, r=8)[:, t],
-                ACT.Copy,
-            )
-
-        def deal_gpsimd(rounded, raw, t):
-            nc.gpsimd.tensor_scalar(
+        def deal_vector(rounded, raw, t):
+            nc.vector.tensor_copy(
                 rounded.rearrange("p (b r j) -> p b r j", r=8, j=PACK),
                 raw[:].rearrange("p j (b t r) -> p t b r j", t=PACK, r=8)[:, t],
-                1.0,
-                0.0,
-                mybir.AluOpType.mult,
-                ADD,
             )
 
         def quantize(rounded, name):
             width = rounded.shape[1] // PACK
             codes = sb([P, width], U32, name + "_codes")
             scales = sb([P, width], U8, name + "_scales")
-            nc.vector.quantize_mx(out=codes[:].bitcast(FP8X4), scales=scales[:], in_=rounded[:])
-            return codes, scales
+            nc.vector.quantize_mx(out=codes[:].bitcast(FP8X4), scales=scales[:], in_=rounded[:, :])
+            return [(codes[:, c : c + P], scales[:, c : c + P]) for c in range(0, width, P)]
 
-        def piece(pair, i):
-            return pair[0][:, i * P : (i + 1) * P], pair[1][:, i * P : (i + 1) * P]
+        def multiply(banks, weights, z):
+            for h in range(2):
+                nc.tensor.matmul_mx(
+                    out=banks[h][:],
+                    lhsT=weights[0].bitcast(FP8X4),
+                    lhsT_scale=weights[1],
+                    rhs=x_codes[z][h].bitcast(FP8X4),
+                    rhs_scale=x_scale[4 * z : P, h * HALF : (h + 1) * HALF],
+                    start=(z == 0),
+                    stop=(z == PASSES - 1),
+                )
 
-        def multiply(bank, weights, z, h):
-            cols = slice(h * HALF, (h + 1) * HALF)
-            nc.tensor.matmul_mx(
-                out=bank[:],
-                lhsT=weights[0].bitcast(FP8X4),
-                lhsT_scale=weights[1],
-                rhs=x_codes[z][:, cols].bitcast(FP8X4),
-                rhs_scale=x_scale[4 * z : P, cols],
-                start=(z == 0),
-                stop=(z == PASSES - 1),
-            )
+        def new_banks():
+            return [psum.tile([P, HALF], F32, name="bank") for h in range(2)]
 
-        def plane(weights, target, copies=(nc.scalar.copy, nc.scalar.copy)):
-            banks = [acc.tile([P, HALF], F32, name="bank") for h in range(2)]
-            for z in range(PASSES):
-                for h in range(2):
-                    multiply(banks[h], weights[z], z, h)
+        def empty(banks, target, copies=(nc.scalar.copy, nc.scalar.copy)):
             for h in range(2):
                 copies[h](target[:, h * HALF : (h + 1) * HALF], banks[h][:])
+            return target
 
-        first = sb([P, PACK * H], BF16, "w1_first")
-        deal_act(first[:, 0:H], w1_raw[0], 0)
-        for t in range(1, PACK):
-            deal_scalar(first[:, t * H : (t + 1) * H], w1_raw[0], t)
-        first_mx = quantize(first, "w1_first")
-        pick_words(1, "w1_raw0")
-        w1_mx = []
-        for t in range(PACK):
-            second = sb([P, H], BF16, f"w1_second{t}")
-            (deal_gpsimd if t == PACK - 1 else deal_scalar)(second[:], w1_raw[1], t)
-            w1_mx.append((piece(first_mx, t), piece(quantize(second, f"w1_second{t}"), 0)))
+        y_banks = []
 
-        y = [sb([P, S], F32, f"y{t}") for t in range(PACK)]
-        plane(w1_mx[0], y[0], (nc.scalar.copy, nc.vector.tensor_copy))
-        for t in (1, 2):
-            plane(w1_mx[t], y[t])
+        def rounded_planes(name, planes):
+            rounded = sb([P, len(planes) * H], BF16, name)
+            for i, (z, t) in enumerate(planes):
+                deal_scalar(rounded[:, i * H : (i + 1) * H], w1_raw[z], t)
+            return rounded
+
+        def open_plane(weights):
+            y_banks.append(new_banks())
+            multiply(y_banks[-1], weights, 0)
+
+        for name, planes in (("w1_a", ((0, 0), (0, 1))), ("w1_b", ((0, 2),))):
+            for weights in quantize(rounded_planes(name, planes), name):
+                open_plane(weights)
+        x_codes.append(pick_words(1, 0, S, "w1_b"))
 
         y_picked = {}
 
-        def pick_y(planes, tag):
-            picked = sb([P, len(planes), S], F32, f"y_picked{planes[0]}", tag)
-            for i, t in enumerate(planes):
-                y_picked[t] = picked[:, i, :]
+        y = sb([P, PACK * S], F32, "y")
+
+        def y_plane(t, width=S):
+            start = (PACK - 1 - t) * S
+            return y[:, start : start + width]
+
+        def pick_y(t, tag=None):
+            y_picked[t] = sb([P, S], F32, f"y_picked{t}", tag)
+            if t == 0:
                 for h in range(2):
                     nc.vector.tensor_copy(
-                        picked[:, i, h * HALF : (h + 1) * HALF],
-                        y[t][:].indirect(src_sb[:, h * HALF // 16 : (h + 1) * HALF // 16]),
+                        y_picked[t][:, h * HALF : (h + 1) * HALF],
+                        y_plane(t).indirect(src_sb[:, h * HALF // 16 : (h + 1) * HALF // 16]),
                     )
+            else:
+                nc.vector.tensor_copy(y_picked[t][:], y_plane(t, 2 * S).indirect(src_sb[:]))
 
-        pick_y((0, 1), None)
-        w2_mx = []
+        mixed = sb([P, 2 * H], BF16, "w1_mixed")
+        deal_scalar(mixed[:, 0:H], w1_raw[0], 3)
+        closing = rounded_planes("w1_c", ((1, 0),))
+        deal_scalar(mixed[:, H : 2 * H], w1_raw[1], 1)
+        third = rounded_planes("w1_d", ((1, 2),))
+        multiply(y_banks[0], quantize(closing, "w1_c")[0], 1)
+        fourth = sb([P, H], BF16, "w1_e", "w1_c")
+        deal_vector(fourth[:], w1_raw[1], 3)
+        mixed_mx = quantize(mixed, "w1_mixed")
+        multiply(y_banks[1], mixed_mx[1], 1)
+        empty(y_banks[0], y_plane(0), (nc.vector.tensor_copy, nc.scalar.copy))
+        multiply(y_banks[2], quantize(third, "w1_d")[0], 1)
+        open_plane(mixed_mx[0])
+        multiply(y_banks[3], quantize(fourth, "w1_e")[0], 1)
+        for t in (1, 2):
+            empty(y_banks[t], y_plane(t))
+        late = sb([P, PACK * PASSES * H], BF16, "late_rounded", "w1_d_codes")
+        for t in range(PACK - 1):
+            pick_y(t)
+
+        e_banks = []
         for t in range(PACK):
-            rounded = sb([P, PASSES * H], BF16, f"w2_rounded{t}")
-            deal_gpsimd(rounded[:, 0:H], w2_raw[0], t)
-            deal_scalar(rounded[:, H : 2 * H], w2_raw[1], t)
-            w2_mx.append(quantize(rounded, f"w2_{t}"))
-        plane(w1_mx[3], y[3])
-        pick_y((2, 3), "w2_raw1")
+            rounded = late[:, PASSES * t * H : PASSES * (t + 1) * H]
+            for z in range(PASSES):
+                deal_scalar(rounded[:, z * H : (z + 1) * H], w2_raw[z], t)
+            e_weights = quantize(rounded, f"w2_{t}")
+            if t == PACK - 1:
+                empty(y_banks[3], y_plane(3))
+                pick_y(3)
+            e_banks.append(new_banks())
+            for z in range(PASSES):
+                multiply(e_banks[t], e_weights[z], z)
+        e = [empty(e_banks[t], sb([P, S], F32, f"e{t}")) for t in range(PACK)]
 
-        e = [sb([P, S], F32, f"e{t}") for t in range(PACK)]
-        for t in range(PACK):
-            plane([piece(w2_mx[t], z) for z in range(PASSES)], e[t])
-
-        w3_rounded = sb([P, PACK * N], BF16, "w3_rounded")
-        nc.gpsimd.tensor_scalar(
-            w3_rounded[:].rearrange("p (c j) -> p c j", j=PACK),
-            w3_raw[:].rearrange("p j c -> p c j"),
-            1.0,
-            0.0,
-            mybir.AluOpType.mult,
-            ADD,
+        w3_rounded = sb([P, PACK * N], BF16, "w3_rounded", "w2_3_codes")
+        nc.scalar.copy(
+            w3_rounded[:].rearrange("p (c i j) -> p c j i", i=4, j=PACK),
+            w3_raw[:].rearrange("p j (c i) -> p c j i", i=4),
         )
         w3_mx = quantize(w3_rounded, "w3")
 
         out_rows = out.rearrange("(m p) r -> p m r", p=P)
+        z_rounded, out_bank = {}, {}
 
-        def edge_values(r0, n):
-            sums = sb([P, PACK, n], F32, f"sums{r0}", "sums", 2)
+        def add(r0, n, tag):
+            sums = sb([P, PACK, n], F32, f"sums{r0}", tag)
             for t in range(PACK):
                 nc.vector.tensor_tensor(
                     sums[:, t, :],
@@ -201,37 +212,56 @@ def tile_picked_hub_relu_p_kernel(
                     y_picked[t][:, r0 : r0 + n],
                     ADD,
                 )
-            z_rounded = sb([P, PACK * n], BF16, f"z{r0}")
+            return sums
+
+        def relu(r0, sums):
+            n = sums.shape[2]
+            z_rounded[r0] = sb([P, PACK * n], BF16, f"z{r0}")
             nc.scalar.activation(
-                z_rounded[:].rearrange("p (c i j) -> p c j i", i=4, j=PACK),
-                sums[:].rearrange("p j (c i) -> p c j i", i=4),
+                z_rounded[r0][:].rearrange("p (c i j) -> p c j i", i=4, j=PACK),
+                sums.rearrange("p j (c i) -> p c j i", i=4),
                 ACT.Relu,
             )
-            return z_rounded
 
-        def finish(r0, z_rounded):
-            n = z_rounded.shape[1] // PACK
-            z_codes, z_scales = quantize(z_rounded, f"z{r0}")
-            bank = fin.tile([P, 2, n], F32, name="out_bank")
+        def last_product(r0):
+            n = z_rounded[r0].shape[1] // PACK
+            z_codes = sb([P, n], U32, f"z_codes{r0}")
+            z_scales = sb([P, n], U8, f"z_scales{r0}")
+            nc.vector.quantize_mx(out=z_codes[:].bitcast(FP8X4), scales=z_scales[:], in_=z_rounded[r0][:])
+            out_bank[r0] = psum.tile([P, 2, n], F32, name="bank")
             for m in range(N // P):
-                codes, scales = piece(w3_mx, m)
                 nc.tensor.matmul_mx(
-                    out=bank[:, m, :],
-                    lhsT=codes.bitcast(FP8X4),
-                    lhsT_scale=scales,
+                    out=out_bank[r0][:, m, :],
+                    lhsT=w3_mx[m][0].bitcast(FP8X4),
+                    lhsT_scale=w3_mx[m][1],
                     rhs=z_codes[:].bitcast(FP8X4),
                     rhs_scale=z_scales[:],
                     start=True,
                     stop=True,
                 )
+
+        def store(r0, copy=nc.scalar.copy):
+            n = out_bank[r0].shape[2]
             result = sb([P, 2, n], F32, f"result{r0}")
-            nc.scalar.copy(result[:], bank[:])
+            copy(result[:], out_bank[r0][:])
             nc.sync.dma_start(out=out_rows[:, :, r0 : r0 + n], in_=result[:])
 
-        starts = [sum(EDGE_CHUNKS[:c]) for c in range(len(EDGE_CHUNKS))]
-        pending = edge_values(starts[0], EDGE_CHUNKS[0])
-        for c in range(1, len(EDGE_CHUNKS)):
-            following = edge_values(starts[c], EDGE_CHUNKS[c])
-            finish(starts[c - 1], pending)
-            pending = following
-        finish(starts[-1], pending)
+        first = add(0, 512, "sums_a")
+        relu(0, first[:, :, 0:256])
+        relu(256, first[:, :, 256:512])
+        relu(512, add(512, 256, "w3_raw")[:])
+        last_product(0)
+        store(0)
+        last_product(256)
+        relu(768, add(768, 128, "sums_a")[:])
+        store(256)
+        last_product(512)
+        store(512)
+        relu(896, add(896, 64, "w3_raw")[:])
+        last_product(768)
+        relu(960, add(960, 64, "sums_a")[:])
+        store(768)
+        last_product(896)
+        store(896)
+        last_product(960)
+        store(960)

@@ -56,16 +56,18 @@ def tile_picked_hub_relu_p_kernel(
             nc.sync.dma_start(out=table[:].bitcast(I32), in_=words)
             return table
 
-        def load_pass(w, z, name):
-            raw = sb([P, PACK, H], F32, name)
-            rows = w[512 * z : 512 * (z + 1), :].rearrange("(p j) c -> p j c", j=PACK)
-            nc.sync.dma_start(out=raw[:], in_=rows)
+        def load_pass(w, z, name, pieces=1):
+            raw = sb([P, PACK * H], F32, name)
+            rows = w[512 * z : 512 * (z + 1), :].rearrange("(p j) c -> p (j c)", j=PACK)
+            width = PACK * H // pieces
+            for c in range(0, PACK * H, width):
+                nc.sync.dma_start(out=raw[:, c : c + width], in_=rows[:, c : c + width])
             return raw
 
         x_word_table, w1_raw = [], []
         for z in range(PASSES):
             x_word_table.append(load_words(z))
-            w1_raw.append(load_pass(w1, z, f"w1_raw{z}"))
+            w1_raw.append(load_pass(w1, z, f"w1_raw{z}", 1 + z))
         nc.sync.dma_start(src_sb[:], src)
         nc.sync.dma_start(dst_sb[:], dst)
         w2_raw = [load_pass(w2, z, f"w2_raw{z}") for z in range(PASSES)]
@@ -87,13 +89,19 @@ def tile_picked_hub_relu_p_kernel(
         def deal_scalar(rounded, raw, t):
             nc.scalar.copy(
                 rounded.rearrange("p (b h r j) -> p b h j r", h=2, r=4, j=PACK),
-                raw[:].rearrange("p j (b t h r) -> p t b h j r", t=PACK, h=2, r=4)[:, t],
+                raw[:].rearrange("p (j b t h r) -> p t b h j r", j=PACK, t=PACK, h=2, r=4)[:, t],
             )
 
         def deal_vector(rounded, raw, t):
             nc.vector.tensor_copy(
                 rounded.rearrange("p (b r j) -> p b r j", r=8, j=PACK),
-                raw[:].rearrange("p j (b t r) -> p t b r j", t=PACK, r=8)[:, t],
+                raw[:].rearrange("p (j b t r) -> p t b r j", j=PACK, t=PACK, r=8)[:, t],
+            )
+
+        def deal_pair(rounded, raw, t, u):
+            nc.scalar.copy(
+                rounded.rearrange("p (b r u e) -> p u b r e", r=8, u=2, e=2)[:, u],
+                raw[:, u * 2 * H : (u + 1) * 2 * H].rearrange("p (e b t r) -> p t b r e", e=2, t=PACK, r=8)[:, t],
             )
 
         def quantize(rounded, name):
@@ -148,8 +156,8 @@ def tile_picked_hub_relu_p_kernel(
             start = (PACK - 1 - t) * S
             return y[:, start : start + width]
 
-        def pick_y(t, tag=None):
-            y_picked[t] = sb([P, S], F32, f"y_picked{t}", tag)
+        def pick_y(t, picked=None):
+            y_picked[t] = sb([P, S], F32, f"y_picked{t}") if picked is None else picked
             if t == 0:
                 for h in range(2):
                     nc.vector.tensor_copy(
@@ -157,11 +165,13 @@ def tile_picked_hub_relu_p_kernel(
                         y_plane(t).indirect(src_sb[:, h * HALF // 16 : (h + 1) * HALF // 16]),
                     )
             else:
-                nc.vector.tensor_copy(y_picked[t][:], y_plane(t, 2 * S).indirect(src_sb[:]))
+                nc.vector.tensor_copy(y_picked[t][:, :], y_plane(t, 2 * S).indirect(src_sb[:]))
 
         mixed = sb([P, 2 * H], BF16, "w1_mixed")
         deal_scalar(mixed[:, 0:H], w1_raw[0], 3)
-        closing = rounded_planes("w1_c", ((1, 0),))
+        closing = sb([P, H], BF16, "w1_c")
+        for u in range(2):
+            deal_pair(closing[:], w1_raw[1], 0, u)
         deal_scalar(mixed[:, H : 2 * H], w1_raw[1], 1)
         third = rounded_planes("w1_d", ((1, 2),))
         multiply(y_banks[0], quantize(closing, "w1_c")[0], 1)
@@ -185,9 +195,9 @@ def tile_picked_hub_relu_p_kernel(
             for z in range(PASSES):
                 deal_scalar(rounded[:, z * H : (z + 1) * H], w2_raw[z], t)
             e_weights = quantize(rounded, f"w2_{t}")
-            if t == PACK - 1:
+            if t == PACK - 2:
                 empty(y_banks[3], y_plane(3))
-                pick_y(3)
+                pick_y(3, late[:, PASSES * H : 3 * PASSES * H].bitcast(F32))
             e_banks.append(new_banks())
             for z in range(PASSES):
                 multiply(e_banks[t], e_weights[z], z)

@@ -104,6 +104,16 @@ def tile_picked_hub_relu_p_kernel(
                 raw[:, u * 2 * H : (u + 1) * 2 * H].rearrange("p (e b t r) -> p t b r e", e=2, t=PACK, r=8)[:, t],
             )
 
+        def deal_gpsimd(rounded, raw, t):
+            nc.gpsimd.tensor_scalar(
+                rounded.rearrange("p (b r j) -> p b r j", r=8, j=PACK),
+                raw[:].rearrange("p (j b t r) -> p t b r j", j=PACK, t=PACK, r=8)[:, t],
+                1.0,
+                0.0,
+                mybir.AluOpType.mult,
+                ADD,
+            )
+
         def quantize(rounded, name):
             width = rounded.shape[1] // PACK
             codes = sb([P, width], U32, name + "_codes")
@@ -192,12 +202,12 @@ def tile_picked_hub_relu_p_kernel(
         e_banks = []
         for t in range(PACK):
             rounded = late[:, PASSES * t * H : PASSES * (t + 1) * H]
-            for z in range(PASSES):
-                deal_scalar(rounded[:, z * H : (z + 1) * H], w2_raw[z], t)
+            deal_gpsimd(rounded[:, 0:H], w2_raw[0], t)
+            deal_scalar(rounded[:, H : 2 * H], w2_raw[1], t)
             e_weights = quantize(rounded, f"w2_{t}")
-            if t == PACK - 2:
+            if t == PACK - 1:
                 empty(y_banks[3], y_plane(3))
-                pick_y(3, late[:, PASSES * H : 3 * PASSES * H].bitcast(F32))
+                pick_y(3, late[:, 2 * PASSES * H : 4 * PASSES * H].bitcast(F32))
             e_banks.append(new_banks())
             for z in range(PASSES):
                 multiply(e_banks[t], e_weights[z], z)

@@ -196,18 +196,31 @@ def tile_picked_hub_relu_p_kernel(
         for t in (1, 2):
             empty(y_banks[t], y_plane(t))
         late = sb([P, PACK * PASSES * H], BF16, "late_rounded", "w1_d_codes")
-        for t in range(PACK - 1):
+        for t in range(2):
             pick_y(t)
+
+        def late_plane(t, count=1):
+            return late[:, PASSES * t * H : PASSES * (t + count) * H]
+
+        def pick_half(h, picked):
+            nc.vector.tensor_copy(
+                picked, y_plane(2, 2 * S).indirect(src_sb[:, h * HALF // 16 : (h + 1) * HALF // 16])
+            )
+            return picked
+
+        y2_halves = [pick_half(0, sb([P, HALF], F32, "y_picked2")[:, :])]
 
         e_banks = []
         for t in range(PACK):
-            rounded = late[:, PASSES * t * H : PASSES * (t + 1) * H]
+            rounded = late_plane(t)
             deal_gpsimd(rounded[:, 0:H], w2_raw[0], t)
             deal_scalar(rounded[:, H : 2 * H], w2_raw[1], t)
             e_weights = quantize(rounded, f"w2_{t}")
+            if t == 1:
+                y2_halves.append(pick_half(1, late_plane(0).bitcast(F32)))
             if t == PACK - 1:
                 empty(y_banks[3], y_plane(3))
-                pick_y(3, late[:, 2 * PASSES * H : 4 * PASSES * H].bitcast(F32))
+                pick_y(3, late_plane(2, 2).bitcast(F32))
             e_banks.append(new_banks())
             for z in range(PASSES):
                 multiply(e_banks[t], e_weights[z], z)
@@ -223,13 +236,18 @@ def tile_picked_hub_relu_p_kernel(
         out_rows = out.rearrange("(m p) r -> p m r", p=P)
         z_rounded, out_bank = {}, {}
 
+        def picked_y(t, r0, n):
+            if t == 2:
+                return y2_halves[r0 // HALF][:, r0 % HALF : r0 % HALF + n]
+            return y_picked[t][:, r0 : r0 + n]
+
         def add(r0, n, tag):
             sums = sb([P, PACK, n], F32, f"sums{r0}", tag)
             for t in range(PACK):
                 nc.vector.tensor_tensor(
                     sums[:, t, :],
                     e[t][:].indirect(dst_sb[:, r0 // 16 : (r0 + n) // 16]),
-                    y_picked[t][:, r0 : r0 + n],
+                    picked_y(t, r0, n),
                     ADD,
                 )
             return sums

@@ -82,7 +82,7 @@ def tile_picked_hub_relu_p_kernel(
         def pick_words(z, c0, n, tag=None):
             codes = sb([P, n], U32, f"x_codes{z}_{c0}", tag)
             nc.vector.tensor_copy(codes[:], x_word_table[z][:].indirect(offs_sb[:, c0 // 16 : (c0 + n) // 16]))
-            return [codes[:, c : c + HALF] for c in range(0, n, HALF)]
+            return codes
 
         x_codes = [pick_words(0, 0, S)]
 
@@ -122,23 +122,25 @@ def tile_picked_hub_relu_p_kernel(
             return [(codes[:, c : c + P], scales[:, c : c + P]) for c in range(0, width, P)]
 
         def multiply(banks, weights, z):
-            for h in range(2):
+            n = S // len(banks)
+            for h, bank in enumerate(banks):
                 nc.tensor.matmul_mx(
-                    out=banks[h][:],
+                    out=bank[:],
                     lhsT=weights[0].bitcast(FP8X4),
                     lhsT_scale=weights[1],
-                    rhs=x_codes[z][h].bitcast(FP8X4),
-                    rhs_scale=x_scale[4 * z : P, h * HALF : (h + 1) * HALF],
+                    rhs=x_codes[z][:, h * n : (h + 1) * n].bitcast(FP8X4),
+                    rhs_scale=x_scale[4 * z : P, h * n : (h + 1) * n],
                     start=(z == 0),
                     stop=(z == PASSES - 1),
                 )
 
-        def new_banks():
-            return [psum.tile([P, HALF], F32, name="bank") for h in range(2)]
+        def new_banks(count=2):
+            return [psum.tile([P, S // count], F32, name="bank") for h in range(count)]
 
         def empty(banks, target, copies=(nc.scalar.copy, nc.scalar.copy)):
-            for h in range(2):
-                copies[h](target[:, h * HALF : (h + 1) * HALF], banks[h][:])
+            n = S // len(banks)
+            for h, bank in enumerate(banks):
+                copies[h % 2](target[:, h * n : (h + 1) * n], bank[:])
             return target
 
         y_banks = []
@@ -150,7 +152,7 @@ def tile_picked_hub_relu_p_kernel(
             return rounded
 
         def open_plane(weights):
-            y_banks.append(new_banks())
+            y_banks.append(new_banks(2 if y_banks else 4))
             multiply(y_banks[-1], weights, 0)
 
         for name, planes in (("w1_a", ((0, 0), (0, 1))), ("w1_b", ((0, 2),))):
@@ -294,12 +296,12 @@ def tile_picked_hub_relu_p_kernel(
         relu(768, add(768, 128, "sums_a")[:])
         store(256)
         last_product(512)
-        store(512)
         relu(896, add(896, 64, "w3_raw")[:])
         last_product(768)
         relu(960, add(960, 64, "sums_a")[:])
-        store(768)
+        store(512)
         last_product(896)
-        store(896)
+        store(768, nc.vector.tensor_copy)
         last_product(960)
-        store(960)
+        store(896)
+        store(960, nc.vector.tensor_copy)

@@ -179,21 +179,19 @@ def tile_picked_hub_relu_p_kernel(
             else:
                 nc.vector.tensor_copy(y_picked[t][:, :], y_plane(t, 2 * S).indirect(src_sb[:]))
 
-        mixed = sb([P, 2 * H], BF16, "w1_mixed")
-        deal_scalar(mixed[:, 0:H], w1_raw[0], 3)
+        last_opening = quantize(rounded_planes("w1_f", ((0, 3),)), "w1_f")[0]
         closing = sb([P, H], BF16, "w1_c")
         for u in range(2):
             deal_pair(closing[:], w1_raw[1], 0, u)
-        deal_scalar(mixed[:, H : 2 * H], w1_raw[1], 1)
+        second = rounded_planes("w1_g", ((1, 1),))
         third = rounded_planes("w1_d", ((1, 2),))
         multiply(y_banks[0], quantize(closing, "w1_c")[0], 1)
         fourth = sb([P, H], BF16, "w1_e", "w1_c")
         deal_vector(fourth[:], w1_raw[1], 3)
-        mixed_mx = quantize(mixed, "w1_mixed")
-        multiply(y_banks[1], mixed_mx[1], 1)
+        multiply(y_banks[1], quantize(second, "w1_g")[0], 1)
         empty(y_banks[0], y_plane(0), (nc.vector.tensor_copy, nc.scalar.copy))
         multiply(y_banks[2], quantize(third, "w1_d")[0], 1)
-        open_plane(mixed_mx[0])
+        open_plane(last_opening)
         multiply(y_banks[3], quantize(fourth, "w1_e")[0], 1)
         for t in (1, 2):
             empty(y_banks[t], y_plane(t))
@@ -212,17 +210,25 @@ def tile_picked_hub_relu_p_kernel(
 
         y2_halves = [pick_half(0, sb([P, HALF], F32, "y_picked2")[:, :])]
 
+        deal_scalar(late_plane(3)[:, 0:H], w2_raw[0], 3)
         e_banks = []
         for t in range(PACK):
             rounded = late_plane(t)
-            deal_gpsimd(rounded[:, 0:H], w2_raw[0], t)
-            deal_scalar(rounded[:, H : 2 * H], w2_raw[1], t)
+            if t < 3:
+                deal_gpsimd(rounded[:, 0:H], w2_raw[0], t)
+            if t < 2:
+                deal_scalar(rounded[:, H : 2 * H], w2_raw[1], t)
+            elif t == 2:
+                nc.scalar.copy(
+                    late_plane(2, 2).rearrange("p (t z b r j) -> p z t b j r", t=2, z=PASSES, r=8, j=PACK)[:, 1],
+                    w2_raw[1][:].rearrange("p (j b u t r) -> p u t b j r", j=PACK, u=2, t=2, r=8)[:, 1],
+                )
             e_weights = quantize(rounded, f"w2_{t}")
             if t == 1:
                 y2_halves.append(pick_half(1, late_plane(0).bitcast(F32)))
             if t == PACK - 1:
                 empty(y_banks[3], y_plane(3))
-                pick_y(3, late_plane(2, 2).bitcast(F32))
+                pick_y(3, late_plane(1, 2).bitcast(F32))
             e_banks.append(new_banks())
             for z in range(PASSES):
                 multiply(e_banks[t], e_weights[z], z)

@@ -12,14 +12,15 @@ U32 = mybir.dt.uint32
 U16 = mybir.dt.uint16
 U8 = mybir.dt.uint8
 FP8X4 = mybir.dt.float8_e4m3fn_x4
-ACT = mybir.ActivationFunctionType
+RELU = mybir.ActivationFunctionType.Relu
 ADD = mybir.AluOpType.add
+MULT = mybir.AluOpType.mult
 
 P = 128
 PACK = 4
 PASSES = K // (P * PACK)
-HALF = 512
-EDGE_CHUNKS = (256, 256, 256, 128, 128)
+HALF = S // 2
+STRIPE = 16
 
 
 def tile_picked_hub_relu_p_kernel(
@@ -34,9 +35,12 @@ def tile_picked_hub_relu_p_kernel(
         def sb(shape, dtype, name, tag=None):
             return keep.tile(shape, dtype, name=name, tag=tag or name, align_bytes=64)
 
-        offs_sb = lists.tile([P, S // 16], U16, name="offs_sb")
-        src_sb = lists.tile([P, S // 16], U16, name="src_sb")
-        dst_sb = lists.tile([P, S // 16], U16, name="dst_sb")
+        def entries(list_tile, first, count):
+            return list_tile[:, first // STRIPE : (first + count) // STRIPE]
+
+        offs_sb = lists.tile([P, S // STRIPE], U16, name="offs_sb")
+        src_sb = lists.tile([P, S // STRIPE], U16, name="src_sb")
+        dst_sb = lists.tile([P, S // STRIPE], U16, name="dst_sb")
 
         x_scale_table = sb([P, T], U8, "x_scale_table")
         nc.vector.memset(x_scale_table[:].bitcast(I32), 0)
@@ -50,27 +54,27 @@ def tile_picked_hub_relu_p_kernel(
             )
             nc.vector.tensor_copy(x_scale_table[rows, :].bitcast(I32), x_scale_rows[rows, :].bitcast(I32))
 
-        def load_words(z):
-            table = sb([P, T], U32, f"x_word_table{z}")
-            words = x_words[z].rearrange("p c r -> p (c r)").bitcast(I32)
+        def load_words(g):
+            table = sb([P, T], U32, f"x_word_table{g}")
+            words = x_words[g].rearrange("p c r -> p (c r)").bitcast(I32)
             nc.sync.dma_start(out=table[:].bitcast(I32), in_=words)
             return table
 
-        def load_pass(w, z, name, pieces=1):
+        def load_pass(w, g, name, pieces=1):
             raw = sb([P, PACK * H], F32, name)
-            rows = w[512 * z : 512 * (z + 1), :].rearrange("(p j) c -> p (j c)", j=PACK)
+            rows = w[P * PACK * g : P * PACK * (g + 1), :].rearrange("(p j) c -> p (j c)", j=PACK)
             width = PACK * H // pieces
             for c in range(0, PACK * H, width):
                 nc.sync.dma_start(out=raw[:, c : c + width], in_=rows[:, c : c + width])
             return raw
 
-        x_word_table, w1_raw = [], []
-        for z in range(PASSES):
-            x_word_table.append(load_words(z))
-            w1_raw.append(load_pass(w1, z, f"w1_raw{z}", 1 + z))
+        x_word_table = [load_words(0)]
+        w1_raw = [load_pass(w1, 0, "w1_raw0")]
+        x_word_table.append(load_words(1))
+        w1_raw.append(load_pass(w1, 1, "w1_raw1", pieces=2))
         nc.sync.dma_start(src_sb[:], src)
         nc.sync.dma_start(dst_sb[:], dst)
-        w2_raw = [load_pass(w2, z, f"w2_raw{z}") for z in range(PASSES)]
+        w2_raw = [load_pass(w2, g, f"w2_raw{g}") for g in range(PASSES)]
         w3_raw = sb([P, PACK, N], F32, "w3_raw")
         w3_rows = w3.rearrange("(b t r) n -> t b r n", t=PACK, r=8)
         for t in range(PACK):
@@ -79,40 +83,43 @@ def tile_picked_hub_relu_p_kernel(
         x_scale = sb([P, S], U8, "x_scale")
         nc.vector.tensor_copy(x_scale[:], x_scale_table[:].indirect(offs_sb[:]))
 
-        def pick_words(z, c0, n, tag=None):
-            codes = sb([P, n], U32, f"x_codes{z}_{c0}", tag)
-            nc.vector.tensor_copy(codes[:], x_word_table[z][:].indirect(offs_sb[:, c0 // 16 : (c0 + n) // 16]))
+        def pick_words(g, tag=None):
+            codes = sb([P, S], U32, f"x_codes{g}", tag)
+            nc.vector.tensor_copy(codes[:], x_word_table[g][:].indirect(offs_sb[:]))
             return codes
 
-        x_codes = [pick_words(0, 0, S)]
+        x_codes = [pick_words(0)]
 
-        def deal_scalar(rounded, raw, t):
-            nc.scalar.copy(
+        def round_plane(copy, rounded, raw, t):
+            copy(
                 rounded.rearrange("p (b h r j) -> p b h j r", h=2, r=4, j=PACK),
                 raw[:].rearrange("p (j b t h r) -> p t b h j r", j=PACK, t=PACK, h=2, r=4)[:, t],
             )
 
-        def deal_vector(rounded, raw, t):
-            nc.vector.tensor_copy(
-                rounded.rearrange("p (b r j) -> p b r j", r=8, j=PACK),
-                raw[:].rearrange("p (j b t r) -> p t b r j", j=PACK, t=PACK, r=8)[:, t],
-            )
+        def round_scalar(rounded, raw, t):
+            round_plane(nc.scalar.copy, rounded, raw, t)
 
-        def deal_pair(rounded, raw, t, u):
+        def round_row_pair(rounded, raw, t, u):
             nc.scalar.copy(
-                rounded.rearrange("p (b r u e) -> p u b r e", r=8, u=2, e=2)[:, u],
-                raw[:, u * 2 * H : (u + 1) * 2 * H].rearrange("p (e b t r) -> p t b r e", e=2, t=PACK, r=8)[:, t],
+                rounded.rearrange("p (b r u v) -> p u b r v", r=8, u=2, v=2)[:, u],
+                raw[:, u * 2 * H : (u + 1) * 2 * H].rearrange("p (v b t r) -> p t b r v", v=2, t=PACK, r=8)[:, t],
             )
 
-        def deal_gpsimd(rounded, raw, t):
+        def round_gpsimd(rounded, raw, t):
             nc.gpsimd.tensor_scalar(
                 rounded.rearrange("p (b r j) -> p b r j", r=8, j=PACK),
                 raw[:].rearrange("p (j b t r) -> p t b r j", j=PACK, t=PACK, r=8)[:, t],
                 1.0,
                 0.0,
-                mybir.AluOpType.mult,
+                MULT,
                 ADD,
             )
+
+        def round_w1(name, g, planes):
+            rounded = sb([P, len(planes) * H], BF16, name)
+            for n, t in enumerate(planes):
+                round_scalar(rounded[:, n * H : (n + 1) * H], w1_raw[g], t)
+            return rounded
 
         def quantize(rounded, name):
             width = rounded.shape[1] // PACK
@@ -121,163 +128,156 @@ def tile_picked_hub_relu_p_kernel(
             nc.vector.quantize_mx(out=codes[:].bitcast(FP8X4), scales=scales[:], in_=rounded[:, :])
             return [(codes[:, c : c + P], scales[:, c : c + P]) for c in range(0, width, P)]
 
-        def multiply(banks, weights, z):
-            n = S // len(banks)
-            for h, bank in enumerate(banks):
+        def multiply(banks, weights, g):
+            width = S // len(banks)
+            for n, bank in enumerate(banks):
                 nc.tensor.matmul_mx(
                     out=bank[:],
                     lhsT=weights[0].bitcast(FP8X4),
                     lhsT_scale=weights[1],
-                    rhs=x_codes[z][:, h * n : (h + 1) * n].bitcast(FP8X4),
-                    rhs_scale=x_scale[4 * z : P, h * n : (h + 1) * n],
-                    start=(z == 0),
-                    stop=(z == PASSES - 1),
+                    rhs=x_codes[g][:, n * width : (n + 1) * width].bitcast(FP8X4),
+                    rhs_scale=x_scale[4 * g : P, n * width : (n + 1) * width],
+                    start=(g == 0),
+                    stop=(g == PASSES - 1),
                 )
 
         def new_banks(count=2):
-            return [psum.tile([P, S // count], F32, name="bank") for h in range(count)]
+            return [psum.tile([P, S // count], F32, name="bank") for n in range(count)]
 
         def empty(banks, target, copies=(nc.scalar.copy, nc.scalar.copy)):
-            n = S // len(banks)
-            for h, bank in enumerate(banks):
-                copies[h % 2](target[:, h * n : (h + 1) * n], bank[:])
+            width = S // len(banks)
+            for n, bank in enumerate(banks):
+                copies[n % 2](target[:, n * width : (n + 1) * width], bank[:])
             return target
 
         y_banks = []
 
-        def rounded_planes(name, planes):
-            rounded = sb([P, len(planes) * H], BF16, name)
-            for i, (z, t) in enumerate(planes):
-                deal_scalar(rounded[:, i * H : (i + 1) * H], w1_raw[z], t)
-            return rounded
-
-        def open_plane(weights):
-            y_banks.append(new_banks(2 if y_banks else 4))
+        def open_plane(weights, count=2):
+            y_banks.append(new_banks(count))
             multiply(y_banks[-1], weights, 0)
 
-        for name, planes in (("w1_a", ((0, 0), (0, 1))), ("w1_b", ((0, 2),))):
-            for weights in quantize(rounded_planes(name, planes), name):
-                open_plane(weights)
-        x_codes.append(pick_words(1, 0, S, "w1_b"))
-
-        y_picked = {}
+        opening = quantize(round_w1("w1_pass0_planes01", 0, (0, 1)), "w1_pass0_planes01")
+        open_plane(opening[0], count=4)
+        open_plane(opening[1])
+        open_plane(quantize(round_w1("w1_pass0_plane2", 0, (2,)), "w1_pass0_plane2")[0])
+        x_codes.append(pick_words(1, "w1_pass0_plane2"))
 
         y = sb([P, PACK * S], F32, "y")
 
         def y_plane(t, width=S):
-            start = (PACK - 1 - t) * S
-            return y[:, start : start + width]
+            first = (PACK - 1 - t) * S
+            return y[:, first : first + width]
 
-        def pick_y(t, picked=None):
-            y_picked[t] = sb([P, S], F32, f"y_picked{t}") if picked is None else picked
-            if t == 0:
-                for h in range(2):
-                    nc.vector.tensor_copy(
-                        y_picked[t][:, h * HALF : (h + 1) * HALF],
-                        y_plane(t).indirect(src_sb[:, h * HALF // 16 : (h + 1) * HALF // 16]),
-                    )
-            else:
-                nc.vector.tensor_copy(y_picked[t][:, :], y_plane(t, 2 * S).indirect(src_sb[:]))
-
-        last_opening = quantize(rounded_planes("w1_f", ((0, 3),)), "w1_f")[0]
-        closing = sb([P, H], BF16, "w1_c")
-        for u in range(2):
-            deal_pair(closing[:], w1_raw[1], 0, u)
-        second = rounded_planes("w1_g", ((1, 1),))
-        third = rounded_planes("w1_d", ((1, 2),))
-        multiply(y_banks[0], quantize(closing, "w1_c")[0], 1)
-        fourth = sb([P, H], BF16, "w1_e", "w1_c")
-        deal_vector(fourth[:], w1_raw[1], 3)
-        multiply(y_banks[1], quantize(second, "w1_g")[0], 1)
-        empty(y_banks[0], y_plane(0), (nc.vector.tensor_copy, nc.scalar.copy))
-        multiply(y_banks[2], quantize(third, "w1_d")[0], 1)
-        open_plane(last_opening)
-        multiply(y_banks[3], quantize(fourth, "w1_e")[0], 1)
-        for t in (1, 2):
-            empty(y_banks[t], y_plane(t))
-        late = sb([P, PACK * PASSES * H], BF16, "late_rounded", "w1_d_codes")
-        for t in range(2):
-            pick_y(t)
-
-        def late_plane(t, count=1):
-            return late[:, PASSES * t * H : PASSES * (t + count) * H]
-
-        def pick_half(h, picked):
-            nc.vector.tensor_copy(
-                picked, y_plane(2, 2 * S).indirect(src_sb[:, h * HALF // 16 : (h + 1) * HALF // 16])
-            )
+        def pick_y(t, picked, first, count):
+            window = y_plane(t) if t == 0 else y_plane(t, 2 * S)
+            nc.vector.tensor_copy(picked, window.indirect(entries(src_sb, first, count)))
             return picked
 
-        y2_halves = [pick_half(0, sb([P, HALF], F32, "y_picked2")[:, :])]
+        plane3_pass0 = quantize(round_w1("w1_pass0_plane3", 0, (3,)), "w1_pass0_plane3")[0]
+        rounded0 = sb([P, H], BF16, "w1_pass1_plane0")
+        for u in range(2):
+            round_row_pair(rounded0[:], w1_raw[1], 0, u)
+        rounded1 = round_w1("w1_pass1_plane1", 1, (1,))
+        rounded2 = round_w1("w1_pass1_plane2", 1, (2,))
+        multiply(y_banks[0], quantize(rounded0, "w1_pass1_plane0")[0], 1)
+        rounded3 = sb([P, H], BF16, "w1_pass1_plane3", "w1_pass1_plane0")
+        round_plane(nc.vector.tensor_copy, rounded3[:], w1_raw[1], 3)
+        multiply(y_banks[1], quantize(rounded1, "w1_pass1_plane1")[0], 1)
+        empty(y_banks[0], y_plane(0), (nc.vector.tensor_copy, nc.scalar.copy))
+        multiply(y_banks[2], quantize(rounded2, "w1_pass1_plane2")[0], 1)
+        open_plane(plane3_pass0)
+        multiply(y_banks[3], quantize(rounded3, "w1_pass1_plane3")[0], 1)
+        for t in (1, 2):
+            empty(y_banks[t], y_plane(t))
 
-        deal_scalar(late_plane(3)[:, 0:H], w2_raw[0], 3)
+        w2_rounded = sb([P, PACK * PASSES * H], BF16, "w2_rounded", "w1_pass1_plane2_codes")
+
+        def w2_planes(t, count=1):
+            return w2_rounded[:, PASSES * t * H : PASSES * (t + count) * H]
+
+        picked0 = sb([P, S], F32, "y_picked0")
+        picked1 = sb([P, S], F32, "y_picked1")
+        y_picked = [
+            [pick_y(0, picked0[:, h * HALF : (h + 1) * HALF], h * HALF, HALF) for h in range(2)],
+        ]
+
+        def halves(picked):
+            return [picked[:, 0:HALF], picked[:, HALF:S]]
+
+        y_picked.append(halves(pick_y(1, picked1[:, :], 0, S)))
+        y_picked.append([pick_y(2, sb([P, HALF], F32, "y_picked2")[:, :], 0, HALF)])
+
+        round_scalar(w2_planes(3)[:, 0:H], w2_raw[0], 3)
         e_banks = []
-        for t in range(PACK):
-            rounded = late_plane(t)
-            if t < 3:
-                deal_gpsimd(rounded[:, 0:H], w2_raw[0], t)
-            if t < 2:
-                deal_scalar(rounded[:, H : 2 * H], w2_raw[1], t)
-            elif t == 2:
-                nc.scalar.copy(
-                    late_plane(2, 2).rearrange("p (t z b r j) -> p z t b j r", t=2, z=PASSES, r=8, j=PACK)[:, 1],
-                    w2_raw[1][:].rearrange("p (j b u t r) -> p u t b j r", j=PACK, u=2, t=2, r=8)[:, 1],
-                )
-            e_weights = quantize(rounded, f"w2_{t}")
-            if t == 1:
-                y2_halves.append(pick_half(1, late_plane(0).bitcast(F32)))
-            if t == PACK - 1:
-                empty(y_banks[3], y_plane(3))
-                pick_y(3, late_plane(1, 2).bitcast(F32))
+
+        def multiply_e(weights):
             e_banks.append(new_banks())
-            for z in range(PASSES):
-                multiply(e_banks[t], e_weights[z], z)
+            for g in range(PASSES):
+                multiply(e_banks[-1], weights[g], g)
+
+        def quantize_w2(t):
+            return quantize(w2_planes(t), f"w2_plane{t}")
+
+        def round_w2(t):
+            round_gpsimd(w2_planes(t)[:, 0:H], w2_raw[0], t)
+            round_scalar(w2_planes(t)[:, H : 2 * H], w2_raw[1], t)
+
+        round_w2(0)
+        multiply_e(quantize_w2(0))
+        round_w2(1)
+        weights = quantize_w2(1)
+        y_picked[2].append(pick_y(2, w2_planes(0).bitcast(F32), HALF, HALF))
+        multiply_e(weights)
+        round_gpsimd(w2_planes(2)[:, 0:H], w2_raw[0], 2)
+        nc.scalar.copy(
+            w2_planes(2, 2).rearrange("p (t g b r j) -> p g t b j r", t=2, g=PASSES, r=8, j=PACK)[:, 1],
+            w2_raw[1][:].rearrange("p (j b u t r) -> p u t b j r", j=PACK, u=2, t=2, r=8)[:, 1],
+        )
+        multiply_e(quantize_w2(2))
+        weights = quantize_w2(3)
+        empty(y_banks[3], y_plane(3))
+        y_picked.append(halves(pick_y(3, w2_planes(1, 2).bitcast(F32), 0, S)))
+        multiply_e(weights)
         e = [empty(e_banks[t], sb([P, S], F32, f"e{t}")) for t in range(PACK)]
 
-        w3_rounded = sb([P, PACK * N], BF16, "w3_rounded", "w2_3_codes")
+        w3_rounded = sb([P, PACK * N], BF16, "w3_rounded", "w2_plane3_codes")
         nc.scalar.copy(
-            w3_rounded[:].rearrange("p (c i j) -> p c j i", i=4, j=PACK),
-            w3_raw[:].rearrange("p j (c i) -> p c j i", i=4),
+            w3_rounded[:].rearrange("p (c r t) -> p c t r", r=4, t=PACK),
+            w3_raw[:].rearrange("p t (c r) -> p c t r", r=4),
         )
         w3_mx = quantize(w3_rounded, "w3")
 
         out_rows = out.rearrange("(m p) r -> p m r", p=P)
         z_rounded, out_bank = {}, {}
 
-        def picked_y(t, r0, n):
-            if t == 2:
-                return y2_halves[r0 // HALF][:, r0 % HALF : r0 % HALF + n]
-            return y_picked[t][:, r0 : r0 + n]
-
-        def add(r0, n, tag):
-            sums = sb([P, PACK, n], F32, f"sums{r0}", tag)
+        def add(first, count, tag):
+            sums = sb([P, PACK, count], F32, f"sums{first}", tag)
             for t in range(PACK):
                 nc.vector.tensor_tensor(
                     sums[:, t, :],
-                    e[t][:].indirect(dst_sb[:, r0 // 16 : (r0 + n) // 16]),
-                    picked_y(t, r0, n),
+                    e[t][:].indirect(entries(dst_sb, first, count)),
+                    y_picked[t][first // HALF][:, first % HALF : first % HALF + count],
                     ADD,
                 )
             return sums
 
-        def relu(r0, sums):
-            n = sums.shape[2]
-            z_rounded[r0] = sb([P, PACK * n], BF16, f"z{r0}")
+        def relu(first, sums):
+            z_rounded[first] = sb([P, PACK * sums.shape[2]], BF16, f"z{first}")
             nc.scalar.activation(
-                z_rounded[r0][:].rearrange("p (c i j) -> p c j i", i=4, j=PACK),
-                sums.rearrange("p j (c i) -> p c j i", i=4),
-                ACT.Relu,
+                z_rounded[first][:].rearrange("p (c r t) -> p c t r", r=4, t=PACK),
+                sums.rearrange("p t (c r) -> p c t r", r=4),
+                RELU,
             )
 
-        def last_product(r0):
-            n = z_rounded[r0].shape[1] // PACK
-            z_codes = sb([P, n], U32, f"z_codes{r0}")
-            z_scales = sb([P, n], U8, f"z_scales{r0}")
-            nc.vector.quantize_mx(out=z_codes[:].bitcast(FP8X4), scales=z_scales[:], in_=z_rounded[r0][:])
-            out_bank[r0] = psum.tile([P, 2, n], F32, name="bank")
+        def last_product(first):
+            count = z_rounded[first].shape[1] // PACK
+            z_codes = sb([P, count], U32, f"z_codes{first}")
+            z_scales = sb([P, count], U8, f"z_scales{first}")
+            nc.vector.quantize_mx(out=z_codes[:].bitcast(FP8X4), scales=z_scales[:], in_=z_rounded[first][:])
+            out_bank[first] = psum.tile([P, N // P, count], F32, name="bank")
             for m in range(N // P):
                 nc.tensor.matmul_mx(
-                    out=out_bank[r0][:, m, :],
+                    out=out_bank[first][:, m, :],
                     lhsT=w3_mx[m][0].bitcast(FP8X4),
                     lhsT_scale=w3_mx[m][1],
                     rhs=z_codes[:].bitcast(FP8X4),
@@ -286,25 +286,25 @@ def tile_picked_hub_relu_p_kernel(
                     stop=True,
                 )
 
-        def store(r0, copy=nc.scalar.copy):
-            n = out_bank[r0].shape[2]
-            result = sb([P, 2, n], F32, f"result{r0}")
-            copy(result[:], out_bank[r0][:])
-            nc.sync.dma_start(out=out_rows[:, :, r0 : r0 + n], in_=result[:])
+        def store(first, copy=nc.scalar.copy):
+            count = out_bank[first].shape[2]
+            result = sb([P, N // P, count], F32, f"result{first}")
+            copy(result[:], out_bank[first][:])
+            nc.sync.dma_start(out=out_rows[:, :, first : first + count], in_=result[:])
 
-        first = add(0, 512, "sums_a")
-        relu(0, first[:, :, 0:256])
-        relu(256, first[:, :, 256:512])
+        sums = add(0, 512, "sums")
+        relu(0, sums[:, :, 0:256])
+        relu(256, sums[:, :, 256:512])
         relu(512, add(512, 256, "w3_raw")[:])
         last_product(0)
         store(0)
         last_product(256)
-        relu(768, add(768, 128, "sums_a")[:])
+        relu(768, add(768, 128, "sums")[:])
         store(256)
         last_product(512)
         relu(896, add(896, 64, "w3_raw")[:])
         last_product(768)
-        relu(960, add(960, 64, "sums_a")[:])
+        relu(960, add(960, 64, "sums")[:])
         store(512)
         last_product(896)
         store(768, nc.vector.tensor_copy)

@@ -12,9 +12,9 @@ U32 = mybir.dt.uint32
 U16 = mybir.dt.uint16
 U8 = mybir.dt.uint8
 FP8X4 = mybir.dt.float8_e4m3fn_x4
+COPY = mybir.ActivationFunctionType.Copy
 RELU = mybir.ActivationFunctionType.Relu
 ADD = mybir.AluOpType.add
-MULT = mybir.AluOpType.mult
 
 P = 128
 PACK = 4
@@ -105,16 +105,6 @@ def tile_picked_hub_relu_p_kernel(
                 raw[:, u * 2 * H : (u + 1) * 2 * H].rearrange("p (v b t r) -> p t b r v", v=2, t=PACK, r=8)[:, t],
             )
 
-        def round_gpsimd(rounded, raw, t):
-            nc.gpsimd.tensor_scalar(
-                rounded.rearrange("p (b r j) -> p b r j", r=8, j=PACK),
-                raw[:].rearrange("p (j b t r) -> p t b r j", j=PACK, t=PACK, r=8)[:, t],
-                1.0,
-                0.0,
-                MULT,
-                ADD,
-            )
-
         def round_w1(name, g, planes):
             rounded = sb([P, len(planes) * H], BF16, name)
             for n, t in enumerate(planes):
@@ -162,17 +152,6 @@ def tile_picked_hub_relu_p_kernel(
         open_plane(quantize(round_w1("w1_pass0_plane2", 0, (2,)), "w1_pass0_plane2")[0])
         x_codes.append(pick_words(1, "w1_pass0_plane2"))
 
-        y = sb([P, PACK * S], F32, "y")
-
-        def y_plane(t, width=S):
-            first = (PACK - 1 - t) * S
-            return y[:, first : first + width]
-
-        def pick_y(t, picked, first, count):
-            window = y_plane(t) if t == 0 else y_plane(t, 2 * S)
-            nc.vector.tensor_copy(picked, window.indirect(entries(src_sb, first, count)))
-            return picked
-
         plane3_pass0 = quantize(round_w1("w1_pass0_plane3", 0, (3,)), "w1_pass0_plane3")[0]
         rounded0 = sb([P, H], BF16, "w1_pass1_plane0")
         for u in range(2):
@@ -183,91 +162,94 @@ def tile_picked_hub_relu_p_kernel(
         rounded3 = sb([P, H], BF16, "w1_pass1_plane3", "w1_pass1_plane0")
         round_plane(nc.vector.tensor_copy, rounded3[:], w1_raw[1], 3)
         multiply(y_banks[1], quantize(rounded1, "w1_pass1_plane1")[0], 1)
-        empty(y_banks[0], y_plane(0), (nc.vector.tensor_copy, nc.scalar.copy))
+        y = [sb([P, S], F32, f"y{t}") for t in range(PACK)]
+        e = [sb([P, S], F32, f"e{t}") for t in range(PACK)]
+        on_scalar = (nc.scalar.copy, nc.scalar.copy)
+        on_vector = (nc.vector.tensor_copy, nc.vector.tensor_copy)
+        empty(y_banks[0], y[0], (nc.vector.tensor_copy, nc.scalar.copy))
         multiply(y_banks[2], quantize(rounded2, "w1_pass1_plane2")[0], 1)
         open_plane(plane3_pass0)
         multiply(y_banks[3], quantize(rounded3, "w1_pass1_plane3")[0], 1)
-        for t in (1, 2):
-            empty(y_banks[t], y_plane(t))
 
-        w2_rounded = sb([P, PACK * PASSES * H], BF16, "w2_rounded", "w1_pass1_plane2_codes")
+        y_picked = [[] for t in range(PACK)]
 
-        def w2_planes(t, count=1):
-            return w2_rounded[:, PASSES * t * H : PASSES * (t + count) * H]
+        def pick_y(t, first, count, picked):
+            nc.scalar.activation(picked, y[t][:].indirect(entries(src_sb, first, count)), COPY)
+            y_picked[t].append((first, picked))
 
-        picked0 = sb([P, S], F32, "y_picked0")
-        picked1 = sb([P, S], F32, "y_picked1")
-        y_picked = [
-            [pick_y(0, picked0[:, h * HALF : (h + 1) * HALF], h * HALF, HALF) for h in range(2)],
-        ]
+        def round_w2(name, g, planes):
+            rounded = sb([P, len(planes) * H], BF16, name)
+            first = planes[0]
+            nc.vector.tensor_copy(
+                rounded[:].rearrange("p (t b r j) -> p t b j r", t=len(planes), r=8, j=PACK),
+                w2_raw[g][:].rearrange("p (j b t r) -> p t b j r", j=PACK, t=PACK, r=8)[:, first : first + len(planes)],
+            )
+            return rounded
 
-        def halves(picked):
-            return [picked[:, 0:HALF], picked[:, HALF:S]]
-
-        y_picked.append(halves(pick_y(1, picked1[:, :], 0, S)))
-        y_picked.append([pick_y(2, sb([P, HALF], F32, "y_picked2")[:, :], 0, HALF)])
-
-        round_scalar(w2_planes(3)[:, 0:H], w2_raw[0], 3)
-        e_banks = []
-
-        def multiply_e(weights):
+        pick_y(0, 0, HALF, sb([P, HALF], F32, "y_picked00")[:, :])
+        empty(y_banks[1], y[1], on_vector)
+        pick_y(1, 0, HALF, sb([P, HALF], F32, "y_picked10")[:, :])
+        w2_pass0_01 = round_w2("w2_pass0_planes01", 0, (0, 1))
+        empty(y_banks[2], y[2], on_scalar)
+        w2_pass1_0 = round_w2("w2_pass1_plane0", 1, (0,))
+        weights = quantize(w2_pass0_01, "w2_pass0_planes01")
+        e_banks = [new_banks() for t in range(2)]
+        for t in range(2):
+            multiply(e_banks[t], weights[t], 0)
+        w2_pass1_1 = round_w2("w2_pass1_plane1", 1, (1,))
+        multiply(e_banks[0], quantize(w2_pass1_0, "w2_pass1_plane0")[0], 1)
+        empty(y_banks[3], y[3], on_scalar)
+        w2_pass0_23 = round_w2("w2_pass0_planes23", 0, (2, 3))
+        multiply(e_banks[1], quantize(w2_pass1_1, "w2_pass1_plane1")[0], 1)
+        w2_pass1_23 = round_w2("w2_pass1_planes23", 1, (2, 3))
+        weights0 = quantize(w2_pass0_23, "w2_pass0_planes23")
+        weights1 = quantize(w2_pass1_23, "w2_pass1_planes23")
+        for t in range(2):
             e_banks.append(new_banks())
-            for g in range(PASSES):
-                multiply(e_banks[-1], weights[g], g)
+            multiply(e_banks[-1], weights0[t], 0)
+            multiply(e_banks[-1], weights1[t], 1)
 
-        def quantize_w2(t):
-            return quantize(w2_planes(t), f"w2_plane{t}")
+        sums = [sb([P, PACK, HALF], F32, f"sums{h}") for h in range(2)]
 
-        def round_w2(t):
-            round_gpsimd(w2_planes(t)[:, 0:H], w2_raw[0], t)
-            round_scalar(w2_planes(t)[:, H : 2 * H], w2_raw[1], t)
+        def add(t, first, count):
+            h, start = divmod(first, HALF)
+            piece, picked = [entry for entry in y_picked[t] if entry[0] <= first][-1]
+            nc.vector.tensor_tensor(
+                sums[h][:, t, start : start + count],
+                e[t][:].indirect(entries(dst_sb, first, count)),
+                picked[:, first - piece : first - piece + count],
+                ADD,
+            )
 
-        round_w2(0)
-        multiply_e(quantize_w2(0))
-        round_w2(1)
-        weights = quantize_w2(1)
-        y_picked[2].append(pick_y(2, w2_planes(0).bitcast(F32), HALF, HALF))
-        multiply_e(weights)
-        round_gpsimd(w2_planes(2)[:, 0:H], w2_raw[0], 2)
-        nc.scalar.copy(
-            w2_planes(2, 2).rearrange("p (t g b r j) -> p g t b j r", t=2, g=PASSES, r=8, j=PACK)[:, 1],
-            w2_raw[1][:].rearrange("p (j b u t r) -> p u t b j r", j=PACK, u=2, t=2, r=8)[:, 1],
-        )
-        multiply_e(quantize_w2(2))
-        weights = quantize_w2(3)
-        empty(y_banks[3], y_plane(3))
-        y_picked.append(halves(pick_y(3, w2_planes(1, 2).bitcast(F32), 0, S)))
-        multiply_e(weights)
-        e = [empty(e_banks[t], sb([P, S], F32, f"e{t}")) for t in range(PACK)]
-
-        w3_rounded = sb([P, PACK * N], BF16, "w3_rounded", "w2_plane3_codes")
-        nc.scalar.copy(
+        empty(e_banks[0], e[0], on_vector)
+        empty(e_banks[1], e[1], on_scalar)
+        pick_y(2, 0, HALF, sb([P, HALF], F32, "y_picked20", "w2_pass1_plane1_codes")[:, :])
+        add(0, 0, HALF)
+        empty(e_banks[2], e[2], on_scalar)
+        add(1, 0, HALF)
+        w3_rounded = sb([P, PACK * N], BF16, "w3_rounded", "y_picked00")
+        nc.vector.tensor_copy(
             w3_rounded[:].rearrange("p (c r t) -> p c t r", r=4, t=PACK),
             w3_raw[:].rearrange("p t (c r) -> p c t r", r=4),
         )
         w3_mx = quantize(w3_rounded, "w3")
+        add(2, 0, HALF)
+        empty(e_banks[3], e[3], (nc.scalar.copy, nc.vector.tensor_copy))
+        pick_y(3, 0, HALF, sb([P, HALF], F32, "y_picked30", "w2_pass1_planes23_codes")[:, :])
+        add(3, 0, HALF)
 
         out_rows = out.rearrange("(m p) r -> p m r", p=P)
         z_rounded, out_bank = {}, {}
 
-        def add(first, count, tag):
-            sums = sb([P, PACK, count], F32, f"sums{first}", tag)
-            for t in range(PACK):
-                nc.vector.tensor_tensor(
-                    sums[:, t, :],
-                    e[t][:].indirect(entries(dst_sb, first, count)),
-                    y_picked[t][first // HALF][:, first % HALF : first % HALF + count],
-                    ADD,
-                )
-            return sums
-
-        def relu(first, sums):
-            z_rounded[first] = sb([P, PACK * sums.shape[2]], BF16, f"z{first}")
-            nc.scalar.activation(
-                z_rounded[first][:].rearrange("p (c r t) -> p c t r", r=4, t=PACK),
-                sums.rearrange("p t (c r) -> p c t r", r=4),
-                RELU,
-            )
+        def relu(first, count, engine):
+            h, start = divmod(first, HALF)
+            z_rounded[first] = sb([P, PACK * count], BF16, f"z{first}")
+            target = z_rounded[first][:].rearrange("p (c r t) -> p c t r", r=4, t=PACK)
+            source = sums[h][:, :, start : start + count].rearrange("p t (c r) -> p c t r", r=4)
+            if engine == "scalar":
+                nc.scalar.activation(target, source, RELU)
+            else:
+                nc.vector.tensor_scalar_max(target, source, 0.0)
 
         def last_product(first):
             count = z_rounded[first].shape[1] // PACK
@@ -292,22 +274,33 @@ def tile_picked_hub_relu_p_kernel(
             copy(result[:], out_bank[first][:])
             nc.sync.dma_start(out=out_rows[:, :, first : first + count], in_=result[:])
 
-        sums = add(0, 512, "sums")
-        relu(0, sums[:, :, 0:256])
-        relu(256, sums[:, :, 256:512])
-        relu(512, add(512, 256, "w3_raw")[:])
+        late01 = sb([P, S], F32, "y_late01", "x_codes0")
+        late23 = sb([P, S], F32, "y_late23", "w2_pass1_planes23_codes")
+        pick_y(0, HALF, HALF, late01[:, 0:HALF])
+        pick_y(1, HALF, HALF, late01[:, HALF:S])
+        relu(0, 256, "scalar")
+        add(0, HALF, HALF)
+        relu(256, 256, "vector")
+        add(1, HALF, HALF)
         last_product(0)
-        store(0)
         last_product(256)
-        relu(768, add(768, 128, "sums")[:])
+        pick_y(2, 512, 256, late23[:, 0:256])
+        pick_y(3, 512, 256, late23[:, 256:512])
+        add(2, 512, 256)
+        add(3, 512, 256)
+        pick_y(2, 768, 256, late23[:, 512:768])
+        pick_y(3, 768, 256, late23[:, 768:1024])
+        store(0)
         store(256)
+        add(2, 768, 256)
+        relu(512, 256, "vector")
+        add(3, 768, 128)
         last_product(512)
-        relu(896, add(896, 64, "w3_raw")[:])
-        last_product(768)
-        relu(960, add(960, 64, "sums")[:])
+        add(3, 896, 128)
+        relu(768, 128, "scalar")
+        relu(896, 128, "vector")
         store(512)
+        last_product(768)
         last_product(896)
-        store(768, nc.vector.tensor_copy)
-        last_product(960)
-        store(896)
-        store(960, nc.vector.tensor_copy)
+        store(768)
+        store(896, nc.vector.tensor_copy)

@@ -76,7 +76,7 @@ def tile_picked_hub_relu_p_kernel(
         nc.sync.dma_start(dst_sb[:], dst)
         w2_raw = [load_pass(w2, g, f"w2_raw{g}") for g in range(PASSES)]
         w3_raw = sb([P, PACK, N], F32, "w3_raw")
-        w3_rows = w3.rearrange("(b t r) n -> t b r n", t=PACK, r=8)
+        w3_rows = w3.rearrange("(m t r) n -> t m r n", t=PACK, r=4)
         for t in range(PACK):
             nc.sync.dma_start(out=w3_raw[:, t, :], in_=w3_rows[t])
 
@@ -92,8 +92,8 @@ def tile_picked_hub_relu_p_kernel(
 
         def round_plane(copy, rounded, raw, t):
             copy(
-                rounded.rearrange("p (b h r j) -> p b h j r", h=2, r=4, j=PACK),
-                raw[:].rearrange("p (j b t h r) -> p t b h j r", j=PACK, t=PACK, h=2, r=4)[:, t],
+                rounded.rearrange("p (m r j) -> p m j r", r=4, j=PACK),
+                raw[:].rearrange("p (j m t r) -> p t m j r", j=PACK, t=PACK, r=4)[:, t],
             )
 
         def round_scalar(rounded, raw, t):
@@ -101,8 +101,8 @@ def tile_picked_hub_relu_p_kernel(
 
         def round_row_pair(rounded, raw, t, u):
             nc.scalar.copy(
-                rounded.rearrange("p (b r u v) -> p u b r v", r=8, u=2, v=2)[:, u],
-                raw[:, u * 2 * H : (u + 1) * 2 * H].rearrange("p (v b t r) -> p t b r v", v=2, t=PACK, r=8)[:, t],
+                rounded.rearrange("p (m r u v) -> p u m v r", r=4, u=2, v=2)[:, u],
+                raw[:, u * 2 * H : (u + 1) * 2 * H].rearrange("p (v m t r) -> p t m v r", v=2, t=PACK, r=4)[:, t],
             )
 
         def round_w1(name, g, planes):
@@ -177,37 +177,36 @@ def tile_picked_hub_relu_p_kernel(
             nc.scalar.activation(picked, y[t][:].indirect(entries(src_sb, first, count)), COPY)
             y_picked[t].append((first, picked))
 
-        def round_w2(name, g, planes):
-            rounded = sb([P, len(planes) * H], BF16, name)
+        def round_w2(rounded, g, planes):
             first = planes[0]
             nc.vector.tensor_copy(
-                rounded[:].rearrange("p (t b r j) -> p t b j r", t=len(planes), r=8, j=PACK),
-                w2_raw[g][:].rearrange("p (j b t r) -> p t b j r", j=PACK, t=PACK, r=8)[:, first : first + len(planes)],
+                rounded.rearrange("p (t m r j) -> p t m j r", t=len(planes), r=4, j=PACK),
+                w2_raw[g][:].rearrange("p (j m t r) -> p t m j r", j=PACK, t=PACK, r=4)[:, first : first + len(planes)],
             )
             return rounded
 
         pick_y(0, 0, HALF, sb([P, HALF], F32, "y_picked00")[:, :])
         empty(y_banks[1], y[1], on_vector)
         pick_y(1, 0, HALF, sb([P, HALF], F32, "y_picked10")[:, :])
-        w2_pass0_01 = round_w2("w2_pass0_planes01", 0, (0, 1))
+        w2_pass0_01 = round_w2(sb([P, 2 * H], BF16, "w2_pass0_planes01")[:, :], 0, (0, 1))
         empty(y_banks[2], y[2], on_scalar)
-        w2_pass1_0 = round_w2("w2_pass1_plane0", 1, (0,))
+        w2_pass1_0 = round_w2(sb([P, H], BF16, "w2_pass1_plane0")[:, :], 1, (0,))
         weights = quantize(w2_pass0_01, "w2_pass0_planes01")
         e_banks = [new_banks() for t in range(2)]
         for t in range(2):
             multiply(e_banks[t], weights[t], 0)
-        w2_pass1_1 = round_w2("w2_pass1_plane1", 1, (1,))
+        w2_pass1_1 = round_w2(sb([P, H], BF16, "w2_pass1_plane1")[:, :], 1, (1,))
         multiply(e_banks[0], quantize(w2_pass1_0, "w2_pass1_plane0")[0], 1)
         empty(y_banks[3], y[3], on_scalar)
-        w2_pass0_23 = round_w2("w2_pass0_planes23", 0, (2, 3))
+        w2_23 = sb([P, 4 * H], BF16, "w2_planes23")
+        round_w2(w2_23[:, 0 : 2 * H], 0, (2, 3))
         multiply(e_banks[1], quantize(w2_pass1_1, "w2_pass1_plane1")[0], 1)
-        w2_pass1_23 = round_w2("w2_pass1_planes23", 1, (2, 3))
-        weights0 = quantize(w2_pass0_23, "w2_pass0_planes23")
-        weights1 = quantize(w2_pass1_23, "w2_pass1_planes23")
+        round_w2(w2_23[:, 2 * H : 4 * H], 1, (2, 3))
+        weights = quantize(w2_23, "w2_planes23")
         for t in range(2):
             e_banks.append(new_banks())
-            multiply(e_banks[-1], weights0[t], 0)
-            multiply(e_banks[-1], weights1[t], 1)
+            multiply(e_banks[-1], weights[t], 0)
+            multiply(e_banks[-1], weights[2 + t], 1)
 
         sums = [sb([P, PACK, HALF], F32, f"sums{h}") for h in range(2)]
 
@@ -235,7 +234,7 @@ def tile_picked_hub_relu_p_kernel(
         w3_mx = quantize(w3_rounded, "w3")
         add(2, 0, HALF)
         empty(e_banks[3], e[3], (nc.scalar.copy, nc.vector.tensor_copy))
-        pick_y(3, 0, HALF, sb([P, HALF], F32, "y_picked30", "w2_pass1_planes23_codes")[:, :])
+        pick_y(3, 0, HALF, sb([P, HALF], F32, "y_picked30", "w2_planes23_codes")[:, :])
         add(3, 0, HALF)
 
         out_rows = out.rearrange("(m p) r -> p m r", p=P)
@@ -274,8 +273,8 @@ def tile_picked_hub_relu_p_kernel(
             copy(result[:], out_bank[first][:])
             nc.sync.dma_start(out=out_rows[:, :, first : first + count], in_=result[:])
 
-        late01 = sb([P, S], F32, "y_late01", "x_codes0")
-        late23 = sb([P, S], F32, "y_late23", "w2_pass1_planes23_codes")
+        late01 = sb([P, S], F32, "y_late01", "w1_pass0_plane2")
+        late23 = sb([P, S], F32, "y_late23", "w2_planes23_codes")
         pick_y(0, HALF, HALF, late01[:, 0:HALF])
         pick_y(1, HALF, HALF, late01[:, HALF:S])
         relu(0, 256, "scalar")

@@ -15,6 +15,7 @@ FP8X4 = mybir.dt.float8_e4m3fn_x4
 COPY = mybir.ActivationFunctionType.Copy
 RELU = mybir.ActivationFunctionType.Relu
 ADD = mybir.AluOpType.add
+MULT = mybir.AluOpType.mult
 
 P = 128
 PACK = 4
@@ -165,7 +166,6 @@ def tile_picked_hub_relu_p_kernel(
         y = [sb([P, S], F32, f"y{t}") for t in range(PACK)]
         e = [sb([P, S], F32, f"e{t}") for t in range(PACK)]
         on_scalar = (nc.scalar.copy, nc.scalar.copy)
-        on_vector = (nc.vector.tensor_copy, nc.vector.tensor_copy)
         empty(y_banks[0], y[0], (nc.vector.tensor_copy, nc.scalar.copy))
         multiply(y_banks[2], quantize(rounded2, "w1_pass1_plane2")[0], 1)
         open_plane(plane3_pass0)
@@ -173,8 +173,12 @@ def tile_picked_hub_relu_p_kernel(
 
         y_picked = [[] for t in range(PACK)]
 
-        def pick_y(t, first, count, picked):
-            nc.scalar.activation(picked, y[t][:].indirect(entries(src_sb, first, count)), COPY)
+        def pick_y(t, first, count, picked, engine="scalar"):
+            window = y[t][:].indirect(entries(src_sb, first, count))
+            if engine == "scalar":
+                nc.scalar.activation(picked, window, COPY)
+            else:
+                nc.vector.tensor_copy(picked, window)
             y_picked[t].append((first, picked))
 
         def round_w2(rounded, g, planes):
@@ -185,28 +189,41 @@ def tile_picked_hub_relu_p_kernel(
             )
             return rounded
 
-        pick_y(0, 0, HALF, sb([P, HALF], F32, "y_picked00")[:, :])
-        empty(y_banks[1], y[1], on_vector)
-        pick_y(1, 0, HALF, sb([P, HALF], F32, "y_picked10")[:, :])
-        w2_pass0_01 = round_w2(sb([P, 2 * H], BF16, "w2_pass0_planes01")[:, :], 0, (0, 1))
+        def round_gpsimd(rounded, t):
+            nc.gpsimd.tensor_scalar(
+                rounded.rearrange("p (m r j) -> p m r j", r=4, j=PACK),
+                w2_raw[0][:].rearrange("p (j m t r) -> p t m r j", j=PACK, t=PACK, r=4)[:, t],
+                1.0,
+                0.0,
+                MULT,
+                ADD,
+            )
+
+        w2_rounded = sb([P, 5 * H], BF16, "w2_rounded", "w1_pass1_plane0")
+        pick_y(0, 0, HALF, sb([P, HALF], F32, "y_picked00")[:, :], "vector")
+        empty(y_banks[1], y[1], on_scalar)
+        pick_y(1, 0, HALF, sb([P, HALF], F32, "y_picked10")[:, :], "vector")
+        round_gpsimd(w2_rounded[:, 3 * H : 4 * H], 0)
+        round_gpsimd(w2_rounded[:, 4 * H : 5 * H], 1)
+        round_gpsimd(w2_rounded[:, 2 * H : 3 * H], 2)
         empty(y_banks[2], y[2], on_scalar)
-        w2_pass1_0 = round_w2(sb([P, H], BF16, "w2_pass1_plane0")[:, :], 1, (0,))
-        weights = quantize(w2_pass0_01, "w2_pass0_planes01")
+        weights = quantize(w2_rounded[:, 3 * H : 5 * H], "w2_pass0_planes01")
         e_banks = [new_banks() for t in range(2)]
         for t in range(2):
             multiply(e_banks[t], weights[t], 0)
+        w2_pass1_0 = round_w2(sb([P, H], BF16, "w2_pass1_plane0")[:, :], 1, (0,))
         w2_pass1_1 = round_w2(sb([P, H], BF16, "w2_pass1_plane1")[:, :], 1, (1,))
         multiply(e_banks[0], quantize(w2_pass1_0, "w2_pass1_plane0")[0], 1)
         empty(y_banks[3], y[3], on_scalar)
-        w2_23 = sb([P, 4 * H], BF16, "w2_planes23")
-        round_w2(w2_23[:, 0 : 2 * H], 0, (2, 3))
+        pick_y(2, 0, HALF, sb([P, HALF], F32, "y_picked20")[:, :])
+        round_w2(w2_rounded[:, 3 * H : 4 * H], 0, (3,))
         multiply(e_banks[1], quantize(w2_pass1_1, "w2_pass1_plane1")[0], 1)
-        round_w2(w2_23[:, 2 * H : 4 * H], 1, (2, 3))
-        weights = quantize(w2_23, "w2_planes23")
+        round_w2(w2_rounded[:, 0 : 2 * H], 1, (2, 3))
+        weights = quantize(w2_rounded[:, 0 : 4 * H], "w2_planes23")
         for t in range(2):
             e_banks.append(new_banks())
-            multiply(e_banks[-1], weights[t], 0)
-            multiply(e_banks[-1], weights[2 + t], 1)
+            multiply(e_banks[-1], weights[2 + t], 0)
+            multiply(e_banks[-1], weights[t], 1)
 
         sums = [sb([P, PACK, HALF], F32, f"sums{h}") for h in range(2)]
 
@@ -220,21 +237,22 @@ def tile_picked_hub_relu_p_kernel(
                 ADD,
             )
 
-        empty(e_banks[0], e[0], on_vector)
-        empty(e_banks[1], e[1], on_scalar)
-        pick_y(2, 0, HALF, sb([P, HALF], F32, "y_picked20", "w2_pass1_plane1_codes")[:, :])
-        add(0, 0, HALF)
-        empty(e_banks[2], e[2], on_scalar)
-        add(1, 0, HALF)
-        w3_rounded = sb([P, PACK * N], BF16, "w3_rounded", "y_picked00")
-        nc.vector.tensor_copy(
-            w3_rounded[:].rearrange("p (c r t) -> p c t r", r=4, t=PACK),
-            w3_raw[:].rearrange("p t (c r) -> p c t r", r=4),
+        pick_y(3, 0, HALF, w2_rounded[:, 0 : 2 * H].bitcast(F32), "vector")
+        w3_rounded = w2_rounded[:, 2 * H : 4 * H]
+        nc.gpsimd.tensor_scalar(
+            w3_rounded.rearrange("p (c t) -> p c t", t=PACK),
+            w3_raw[:].rearrange("p t c -> p c t"),
+            1.0,
+            0.0,
+            MULT,
+            ADD,
         )
+        for t in range(PACK):
+            empty(e_banks[t], e[t], on_scalar)
+        add(0, 0, HALF)
+        add(1, 0, HALF)
         w3_mx = quantize(w3_rounded, "w3")
         add(2, 0, HALF)
-        empty(e_banks[3], e[3], (nc.scalar.copy, nc.vector.tensor_copy))
-        pick_y(3, 0, HALF, sb([P, HALF], F32, "y_picked30", "w2_planes23_codes")[:, :])
         add(3, 0, HALF)
 
         out_rows = out.rearrange("(m p) r -> p m r", p=P)
@@ -274,7 +292,7 @@ def tile_picked_hub_relu_p_kernel(
             nc.sync.dma_start(out=out_rows[:, :, first : first + count], in_=result[:])
 
         late01 = sb([P, S], F32, "y_late01", "w1_pass0_plane2")
-        late23 = sb([P, S], F32, "y_late23", "w2_planes23_codes")
+        late23 = sb([P, S], F32, "y_late23", "y_picked20")
         pick_y(0, HALF, HALF, late01[:, 0:HALF])
         pick_y(1, HALF, HALF, late01[:, HALF:S])
         relu(0, 256, "scalar")
@@ -290,16 +308,16 @@ def tile_picked_hub_relu_p_kernel(
         pick_y(2, 768, 256, late23[:, 512:768])
         pick_y(3, 768, 256, late23[:, 768:1024])
         store(0)
-        store(256)
         add(2, 768, 256)
-        relu(512, 256, "vector")
+        relu(512, 256, "scalar")
         add(3, 768, 128)
-        last_product(512)
         add(3, 896, 128)
-        relu(768, 128, "scalar")
+        store(256)
+        relu(768, 128, "vector")
         relu(896, 128, "vector")
-        store(512)
+        last_product(512)
         last_product(768)
         last_product(896)
+        store(512)
         store(768)
         store(896, nc.vector.tensor_copy)

@@ -15,7 +15,6 @@ FP8X4 = mybir.dt.float8_e4m3fn_x4
 COPY = mybir.ActivationFunctionType.Copy
 RELU = mybir.ActivationFunctionType.Relu
 ADD = mybir.AluOpType.add
-MULT = mybir.AluOpType.mult
 
 P = 128
 PACK = 4
@@ -112,9 +111,9 @@ def tile_picked_hub_relu_p_kernel(
                 round_scalar(rounded[:, n * H : (n + 1) * H], w1_raw[g], t)
             return rounded
 
-        def quantize(rounded, name):
+        def quantize(rounded, name, tag=None):
             width = rounded.shape[1] // PACK
-            codes = sb([P, width], U32, name + "_codes")
+            codes = sb([P, width], U32, name + "_codes", tag)
             scales = sb([P, width], U8, name + "_scales")
             nc.vector.quantize_mx(out=codes[:].bitcast(FP8X4), scales=scales[:], in_=rounded[:, :])
             return [(codes[:, c : c + P], scales[:, c : c + P]) for c in range(0, width, P)]
@@ -189,25 +188,14 @@ def tile_picked_hub_relu_p_kernel(
             )
             return rounded
 
-        def round_gpsimd(rounded, t):
-            nc.gpsimd.tensor_scalar(
-                rounded.rearrange("p (m r j) -> p m r j", r=4, j=PACK),
-                w2_raw[0][:].rearrange("p (j m t r) -> p t m r j", j=PACK, t=PACK, r=4)[:, t],
-                1.0,
-                0.0,
-                MULT,
-                ADD,
-            )
-
-        w2_rounded = sb([P, 5 * H], BF16, "w2_rounded", "w1_pass1_plane0")
         pick_y(0, 0, HALF, sb([P, HALF], F32, "y_picked00")[:, :], "vector")
         empty(y_banks[1], y[1], on_scalar)
-        pick_y(1, 0, HALF, sb([P, HALF], F32, "y_picked10")[:, :], "vector")
-        round_gpsimd(w2_rounded[:, 3 * H : 4 * H], 0)
-        round_gpsimd(w2_rounded[:, 4 * H : 5 * H], 1)
-        round_gpsimd(w2_rounded[:, 2 * H : 3 * H], 2)
+        w2_pass0_01 = round_w2(sb([P, 2 * H], BF16, "w2_pass0_planes01")[:, :], 0, (0, 1))
         empty(y_banks[2], y[2], on_scalar)
-        weights = quantize(w2_rounded[:, 3 * H : 5 * H], "w2_pass0_planes01")
+        pick_y(1, 0, HALF, sb([P, HALF], F32, "y_picked10")[:, :])
+        w2_23 = sb([P, 4 * H], BF16, "w2_planes23")
+        round_w2(w2_23[:, 0 : 2 * H], 0, (2, 3))
+        weights = quantize(w2_pass0_01, "w2_pass0_planes01")
         e_banks = [new_banks() for t in range(2)]
         for t in range(2):
             multiply(e_banks[t], weights[t], 0)
@@ -215,54 +203,47 @@ def tile_picked_hub_relu_p_kernel(
         w2_pass1_1 = round_w2(sb([P, H], BF16, "w2_pass1_plane1")[:, :], 1, (1,))
         multiply(e_banks[0], quantize(w2_pass1_0, "w2_pass1_plane0")[0], 1)
         empty(y_banks[3], y[3], on_scalar)
-        pick_y(2, 0, HALF, sb([P, HALF], F32, "y_picked20")[:, :])
-        round_w2(w2_rounded[:, 3 * H : 4 * H], 0, (3,))
         multiply(e_banks[1], quantize(w2_pass1_1, "w2_pass1_plane1")[0], 1)
-        round_w2(w2_rounded[:, 0 : 2 * H], 1, (2, 3))
-        weights = quantize(w2_rounded[:, 0 : 4 * H], "w2_planes23")
+        round_w2(w2_23[:, 2 * H : 4 * H], 1, (2, 3))
+        w3_rounded = sb([P, PACK * N], BF16, "w3_rounded", "w2_pass1_plane1")
+        nc.vector.tensor_copy(
+            w3_rounded[:].rearrange("p (c r t) -> p c t r", r=4, t=PACK),
+            w3_raw[:].rearrange("p t (c r) -> p c t r", r=4),
+        )
+        weights = quantize(w2_23, "w2_planes23")
         for t in range(2):
             e_banks.append(new_banks())
-            multiply(e_banks[-1], weights[2 + t], 0)
-            multiply(e_banks[-1], weights[t], 1)
+            multiply(e_banks[-1], weights[t], 0)
+            multiply(e_banks[-1], weights[2 + t], 1)
 
-        sums = [sb([P, PACK, HALF], F32, f"sums{h}") for h in range(2)]
+        sums = [sb([P, PACK * HALF], F32, f"sums{h}") for h in range(2)]
 
         def add(t, first, count):
             h, start = divmod(first, HALF)
             piece, picked = [entry for entry in y_picked[t] if entry[0] <= first][-1]
             nc.vector.tensor_tensor(
-                sums[h][:, t, start : start + count],
+                sums[h][:, t * HALF + start : t * HALF + start + count],
                 e[t][:].indirect(entries(dst_sb, first, count)),
                 picked[:, first - piece : first - piece + count],
                 ADD,
             )
 
-        pick_y(3, 0, HALF, w2_rounded[:, 0 : 2 * H].bitcast(F32), "vector")
-        w3_rounded = w2_rounded[:, 2 * H : 4 * H]
-        nc.gpsimd.tensor_scalar(
-            w3_rounded.rearrange("p (c t) -> p c t", t=PACK),
-            w3_raw[:].rearrange("p t c -> p c t"),
-            1.0,
-            0.0,
-            MULT,
-            ADD,
-        )
-        for t in range(PACK):
+        pick_y(2, 0, HALF, w2_23[:, 0 : 2 * H].bitcast(F32), "vector")
+        for t in range(3):
             empty(e_banks[t], e[t], on_scalar)
-        add(0, 0, HALF)
-        add(1, 0, HALF)
-        w3_mx = quantize(w3_rounded, "w3")
-        add(2, 0, HALF)
-        add(3, 0, HALF)
+        pick_y(3, 0, HALF, sb([P, HALF], F32, "y_picked30", "w2_planes23_codes")[:, :])
+        empty(e_banks[3], e[3], on_scalar)
+        for t in range(PACK):
+            add(t, 0, HALF)
 
         out_rows = out.rearrange("(m p) r -> p m r", p=P)
         z_rounded, out_bank = {}, {}
 
-        def relu(first, count, engine):
+        def relu(first, count, engine, rounded=None):
             h, start = divmod(first, HALF)
-            z_rounded[first] = sb([P, PACK * count], BF16, f"z{first}")
-            target = z_rounded[first][:].rearrange("p (c r t) -> p c t r", r=4, t=PACK)
-            source = sums[h][:, :, start : start + count].rearrange("p t (c r) -> p c t r", r=4)
+            z_rounded[first] = sb([P, PACK * count], BF16, f"z{first}")[:, :] if rounded is None else rounded
+            target = z_rounded[first].rearrange("p (c r t) -> p c t r", r=4, t=PACK)
+            source = sums[h][:].rearrange("p (t c r) -> p c t r", t=PACK, r=4)[:, start // 4 : (start + count) // 4]
             if engine == "scalar":
                 nc.scalar.activation(target, source, RELU)
             else:
@@ -272,7 +253,7 @@ def tile_picked_hub_relu_p_kernel(
             count = z_rounded[first].shape[1] // PACK
             z_codes = sb([P, count], U32, f"z_codes{first}")
             z_scales = sb([P, count], U8, f"z_scales{first}")
-            nc.vector.quantize_mx(out=z_codes[:].bitcast(FP8X4), scales=z_scales[:], in_=z_rounded[first][:])
+            nc.vector.quantize_mx(out=z_codes[:].bitcast(FP8X4), scales=z_scales[:], in_=z_rounded[first])
             out_bank[first] = psum.tile([P, N // P, count], F32, name="bank")
             for m in range(N // P):
                 nc.tensor.matmul_mx(
@@ -285,37 +266,39 @@ def tile_picked_hub_relu_p_kernel(
                     stop=True,
                 )
 
-        def store(first, copy=nc.scalar.copy):
+        def store(first, copy=nc.scalar.copy, result=None):
             count = out_bank[first].shape[2]
-            result = sb([P, N // P, count], F32, f"result{first}")
-            copy(result[:], out_bank[first][:])
-            nc.sync.dma_start(out=out_rows[:, :, first : first + count], in_=result[:])
+            if result is None:
+                result = sb([P, N // P, count], F32, f"result{first}")[:, :, :]
+            copy(result, out_bank[first][:])
+            nc.sync.dma_start(out=out_rows[:, :, first : first + count], in_=result)
 
         late01 = sb([P, S], F32, "y_late01", "w1_pass0_plane2")
-        late23 = sb([P, S], F32, "y_late23", "y_picked20")
+        late23 = sb([P, HALF], F32, "y_late23", "x_codes0")
         pick_y(0, HALF, HALF, late01[:, 0:HALF])
         pick_y(1, HALF, HALF, late01[:, HALF:S])
         relu(0, 256, "scalar")
         add(0, HALF, HALF)
         relu(256, 256, "vector")
-        add(1, HALF, HALF)
-        last_product(0)
+        w3_mx = quantize(w3_rounded, "w3", "w2_planes23_codes")
         last_product(256)
+        last_product(0)
+        add(1, HALF, HALF)
         pick_y(2, 512, 256, late23[:, 0:256])
         pick_y(3, 512, 256, late23[:, 256:512])
+        store(256)
         add(2, 512, 256)
         add(3, 512, 256)
-        pick_y(2, 768, 256, late23[:, 512:768])
-        pick_y(3, 768, 256, late23[:, 768:1024])
-        store(0)
+        last23 = sb([P, HALF], F32, "y_last23", "z_codes256")
+        pick_y(2, 768, 256, last23[:, 0:256])
+        pick_y(3, 768, 256, last23[:, 256:512])
         add(2, 768, 256)
         relu(512, 256, "scalar")
-        add(3, 768, 128)
-        add(3, 896, 128)
-        store(256)
-        relu(768, 128, "vector")
-        relu(896, 128, "vector")
+        add(3, 768, 256)
+        store(0, result=sums[1][:].rearrange("p (t c) -> p t c", t=PACK)[:, 2:4, 0:256])
         last_product(512)
+        relu(768, 128, "vector", sums[1][:, 0:256].bitcast(BF16))
+        relu(896, 128, "vector", sums[1][:, HALF : HALF + 256].bitcast(BF16))
         last_product(768)
         last_product(896)
         store(512)

@@ -20,6 +20,7 @@ P = 128
 PACK = 4
 PASSES = K // (P * PACK)
 HALF = S // 2
+SPARE = 16
 STRIPE = 16
 
 
@@ -111,9 +112,9 @@ def tile_picked_hub_relu_p_kernel(
                 round_scalar(rounded[:, n * H : (n + 1) * H], w1_raw[g], t)
             return rounded
 
-        def quantize(rounded, name, tag=None):
+        def quantize(rounded, name):
             width = rounded.shape[1] // PACK
-            codes = sb([P, width], U32, name + "_codes", tag)
+            codes = sb([P, width], U32, name + "_codes")
             scales = sb([P, width], U8, name + "_scales")
             nc.vector.quantize_mx(out=codes[:].bitcast(FP8X4), scales=scales[:], in_=rounded[:, :])
             return [(codes[:, c : c + P], scales[:, c : c + P]) for c in range(0, width, P)]
@@ -162,8 +163,10 @@ def tile_picked_hub_relu_p_kernel(
         rounded3 = sb([P, H], BF16, "w1_pass1_plane3", "w1_pass1_plane0")
         round_plane(nc.vector.tensor_copy, rounded3[:], w1_raw[1], 3)
         multiply(y_banks[1], quantize(rounded1, "w1_pass1_plane1")[0], 1)
-        y = [sb([P, S], F32, f"y{t}") for t in range(PACK)]
-        e = [sb([P, S], F32, f"e{t}") for t in range(PACK)]
+        y = [sb([P, S + SPARE if t == 1 else S], F32, f"y{t}") for t in range(PACK - 1)]
+        e = [sb([P, S + SPARE if t < 2 else S], F32, f"e{t}") for t in range(PACK)]
+        for window in (y[1], e[0], e[1]):
+            nc.gpsimd.memset(window[:, S : S + SPARE], 0.0)
         on_scalar = (nc.scalar.copy, nc.scalar.copy)
         empty(y_banks[0], y[0], (nc.vector.tensor_copy, nc.scalar.copy))
         multiply(y_banks[2], quantize(rounded2, "w1_pass1_plane2")[0], 1)
@@ -188,11 +191,14 @@ def tile_picked_hub_relu_p_kernel(
             )
             return rounded
 
-        pick_y(0, 0, HALF, sb([P, HALF], F32, "y_picked00")[:, :], "vector")
+        picked0 = sb([P, S], F32, "y_picked0")
+        pick_y(0, 0, HALF, picked0[:, 0:HALF], "vector")
         empty(y_banks[1], y[1], on_scalar)
         w2_pass0_01 = round_w2(sb([P, 2 * H], BF16, "w2_pass0_planes01")[:, :], 0, (0, 1))
-        empty(y_banks[2], y[2], on_scalar)
-        pick_y(1, 0, HALF, sb([P, HALF], F32, "y_picked10")[:, :])
+        nc.scalar.copy(y[2][:, 0:HALF], y_banks[2][0][:])
+        pick_y(0, HALF, HALF, picked0[:, HALF:S])
+        y_picked[0] = [(0, picked0[:, :])]
+        pick_y(1, 0, S, sb([P, S], F32, "y_picked1")[:, :])
         w2_23 = sb([P, 4 * H], BF16, "w2_planes23")
         round_w2(w2_23[:, 0 : 2 * H], 0, (2, 3))
         weights = quantize(w2_pass0_01, "w2_pass0_planes01")
@@ -202,7 +208,6 @@ def tile_picked_hub_relu_p_kernel(
         w2_pass1_0 = round_w2(sb([P, H], BF16, "w2_pass1_plane0")[:, :], 1, (0,))
         w2_pass1_1 = round_w2(sb([P, H], BF16, "w2_pass1_plane1")[:, :], 1, (1,))
         multiply(e_banks[0], quantize(w2_pass1_0, "w2_pass1_plane0")[0], 1)
-        empty(y_banks[3], y[3], on_scalar)
         multiply(e_banks[1], quantize(w2_pass1_1, "w2_pass1_plane1")[0], 1)
         round_w2(w2_23[:, 2 * H : 4 * H], 1, (2, 3))
         w3_rounded = sb([P, PACK * N], BF16, "w3_rounded", "w2_pass1_plane1")
@@ -210,40 +215,45 @@ def tile_picked_hub_relu_p_kernel(
             w3_rounded[:].rearrange("p (c r t) -> p c t r", r=4, t=PACK),
             w3_raw[:].rearrange("p t (c r) -> p c t r", r=4),
         )
+        nc.vector.tensor_copy(y[2][:, HALF:S], y_banks[2][1][:])
         weights = quantize(w2_23, "w2_planes23")
+        for t in range(2):
+            empty(e_banks[t], e[t], on_scalar)
+        y.append(sb([P, S], F32, "y3", "w2_pass1_plane1_codes"))
+        empty(y_banks[3], y[3], (nc.vector.tensor_copy, nc.scalar.copy))
         for t in range(2):
             e_banks.append(new_banks())
             multiply(e_banks[-1], weights[t], 0)
             multiply(e_banks[-1], weights[2 + t], 1)
+        w3_mx = quantize(w3_rounded, "w3")
 
-        sums = [sb([P, PACK * HALF], F32, f"sums{h}") for h in range(2)]
+        sums = sb([P, PACK * S], F32, "sums")
 
         def add(t, first, count):
-            h, start = divmod(first, HALF)
             piece, picked = [entry for entry in y_picked[t] if entry[0] <= first][-1]
             nc.vector.tensor_tensor(
-                sums[h][:, t * HALF + start : t * HALF + start + count],
+                sums[:, t * S + first : t * S + first + count],
                 e[t][:].indirect(entries(dst_sb, first, count)),
                 picked[:, first - piece : first - piece + count],
                 ADD,
             )
 
-        pick_y(2, 0, HALF, w2_23[:, 0 : 2 * H].bitcast(F32), "vector")
-        for t in range(3):
-            empty(e_banks[t], e[t], on_scalar)
-        pick_y(3, 0, HALF, sb([P, HALF], F32, "y_picked30", "w2_planes23_codes")[:, :])
+        pick_y(2, 0, HALF, sb([P, HALF], F32, "y_picked20", "w2_pass1_plane0_codes")[:, :])
+        empty(e_banks[2], e[2], on_scalar)
+        pick_y(3, 0, HALF, sb([P, HALF], F32, "y_picked30")[:, :])
         empty(e_banks[3], e[3], on_scalar)
-        for t in range(PACK):
+        for t in range(2):
+            add(t, 0, S)
+        for t in range(2, PACK):
             add(t, 0, HALF)
 
         out_rows = out.rearrange("(m p) r -> p m r", p=P)
         z_rounded, out_bank = {}, {}
 
         def relu(first, count, engine, rounded=None):
-            h, start = divmod(first, HALF)
             z_rounded[first] = sb([P, PACK * count], BF16, f"z{first}")[:, :] if rounded is None else rounded
             target = z_rounded[first].rearrange("p (c r t) -> p c t r", r=4, t=PACK)
-            source = sums[h][:].rearrange("p (t c r) -> p c t r", t=PACK, r=4)[:, start // 4 : (start + count) // 4]
+            source = sums[:].rearrange("p (t c r) -> p c t r", t=PACK, r=4)[:, first // 4 : (first + count) // 4]
             if engine == "scalar":
                 nc.scalar.activation(target, source, RELU)
             else:
@@ -266,39 +276,29 @@ def tile_picked_hub_relu_p_kernel(
                     stop=True,
                 )
 
-        def store(first, copy=nc.scalar.copy, result=None):
+        def store(first, copy=nc.scalar.copy):
             count = out_bank[first].shape[2]
-            if result is None:
-                result = sb([P, N // P, count], F32, f"result{first}")[:, :, :]
-            copy(result, out_bank[first][:])
-            nc.sync.dma_start(out=out_rows[:, :, first : first + count], in_=result)
+            result = sb([P, N // P, count], F32, f"result{first}")
+            copy(result[:], out_bank[first][:])
+            nc.sync.dma_start(out=out_rows[:, :, first : first + count], in_=result[:])
 
-        late01 = sb([P, S], F32, "y_late01", "w1_pass0_plane2")
-        late23 = sb([P, HALF], F32, "y_late23", "x_codes0")
-        pick_y(0, HALF, HALF, late01[:, 0:HALF])
-        pick_y(1, HALF, HALF, late01[:, HALF:S])
+        late23 = sb([P, S], F32, "y_late23", "w1_pass0_plane2")
+        pick_y(2, HALF, HALF, late23[:, 0:HALF])
+        pick_y(3, HALF, HALF, late23[:, HALF:S])
         relu(0, 256, "scalar")
-        add(0, HALF, HALF)
-        relu(256, 256, "vector")
-        w3_mx = quantize(w3_rounded, "w3", "w2_planes23_codes")
-        last_product(256)
-        last_product(0)
-        add(1, HALF, HALF)
-        pick_y(2, 512, 256, late23[:, 0:256])
-        pick_y(3, 512, 256, late23[:, 256:512])
-        store(256)
         add(2, 512, 256)
+        relu(256, 256, "vector")
         add(3, 512, 256)
-        last23 = sb([P, HALF], F32, "y_last23", "z_codes256")
-        pick_y(2, 768, 256, last23[:, 0:256])
-        pick_y(3, 768, 256, last23[:, 256:512])
-        add(2, 768, 256)
         relu(512, 256, "scalar")
+        last_product(256)
+        add(2, 768, 256)
+        last_product(0)
         add(3, 768, 256)
-        store(0, result=sums[1][:].rearrange("p (t c) -> p t c", t=PACK)[:, 2:4, 0:256])
+        store(256)
+        store(0)
         last_product(512)
-        relu(768, 128, "vector", sums[1][:, 0:256].bitcast(BF16))
-        relu(896, 128, "vector", sums[1][:, HALF : HALF + 256].bitcast(BF16))
+        relu(768, 128, "vector", sums[:, 512:768].bitcast(BF16))
+        relu(896, 128, "vector", sums[:, S + 512 : S + 768].bitcast(BF16))
         last_product(768)
         last_product(896)
         store(512)

@@ -74,8 +74,8 @@ def tile_picked_hub_relu_p_kernel(
         x_word_table.append(load_words(1))
         w1_raw.append(load_pass(w1, 1, "w1_raw1", pieces=2))
         nc.sync.dma_start(src_sb[:], src)
-        nc.sync.dma_start(dst_sb[:], dst)
         w2_raw = [load_pass(w2, g, f"w2_raw{g}") for g in range(PASSES)]
+        nc.sync.dma_start(dst_sb[:], dst)
         w3_raw = sb([P, PACK, N], F32, "w3_raw")
         w3_rows = w3.rearrange("(m t r) n -> t m r n", t=PACK, r=4)
         for t in range(PACK):
@@ -195,7 +195,7 @@ def tile_picked_hub_relu_p_kernel(
         pick_y(0, 0, HALF, picked0[:, 0:HALF], "vector")
         empty(y_banks[1], y[1], on_scalar)
         w2_pass0_01 = round_w2(sb([P, 2 * H], BF16, "w2_pass0_planes01")[:, :], 0, (0, 1))
-        nc.scalar.copy(y[2][:, 0:HALF], y_banks[2][0][:])
+        empty(y_banks[2], y[2], on_scalar)
         pick_y(0, HALF, HALF, picked0[:, HALF:S])
         y_picked[0] = [(0, picked0[:, :])]
         pick_y(1, 0, S, sb([P, S], F32, "y_picked1")[:, :])
@@ -210,24 +210,17 @@ def tile_picked_hub_relu_p_kernel(
         multiply(e_banks[0], quantize(w2_pass1_0, "w2_pass1_plane0")[0], 1)
         multiply(e_banks[1], quantize(w2_pass1_1, "w2_pass1_plane1")[0], 1)
         round_w2(w2_23[:, 2 * H : 4 * H], 1, (2, 3))
-        w3_rounded = sb([P, PACK * N], BF16, "w3_rounded", "w2_pass1_plane1")
-        nc.vector.tensor_copy(
-            w3_rounded[:].rearrange("p (c r t) -> p c t r", r=4, t=PACK),
-            w3_raw[:].rearrange("p t (c r) -> p c t r", r=4),
-        )
-        nc.vector.tensor_copy(y[2][:, HALF:S], y_banks[2][1][:])
         weights = quantize(w2_23, "w2_planes23")
-        for t in range(2):
-            empty(e_banks[t], e[t], on_scalar)
-        y.append(sb([P, S], F32, "y3", "w2_pass1_plane1_codes"))
-        empty(y_banks[3], y[3], (nc.vector.tensor_copy, nc.scalar.copy))
+        empty(e_banks[0], e[0], on_scalar)
+        y.append(sb([P, S], F32, "y3", "w2_pass1_plane0_codes"))
+        empty(y_banks[3], y[3], on_scalar)
+        empty(e_banks[1], e[1], on_scalar)
         for t in range(2):
             e_banks.append(new_banks())
             multiply(e_banks[-1], weights[t], 0)
             multiply(e_banks[-1], weights[2 + t], 1)
-        w3_mx = quantize(w3_rounded, "w3")
 
-        sums = sb([P, PACK * S], F32, "sums")
+        sums = sb([P, PACK * S], F32, "sums", "w3_raw")
 
         def add(t, first, count):
             piece, picked = [entry for entry in y_picked[t] if entry[0] <= first][-1]
@@ -238,7 +231,13 @@ def tile_picked_hub_relu_p_kernel(
                 ADD,
             )
 
-        pick_y(2, 0, HALF, sb([P, HALF], F32, "y_picked20", "w2_pass1_plane0_codes")[:, :])
+        w3_rounded = w2_23[:, 0 : PACK * N]
+        nc.vector.tensor_copy(
+            w3_rounded.rearrange("p (c r t) -> p c t r", r=4, t=PACK),
+            w3_raw[:].rearrange("p t (c r) -> p c t r", r=4),
+        )
+        pick_y(2, 0, HALF, sb([P, HALF], F32, "y_picked20", "w2_pass1_plane1")[:, :], "vector")
+        w3_mx = quantize(w3_rounded, "w3")
         empty(e_banks[2], e[2], on_scalar)
         pick_y(3, 0, HALF, sb([P, HALF], F32, "y_picked30")[:, :])
         empty(e_banks[3], e[3], on_scalar)

from contextlib import ExitStack

import concourse.mybir as mybir

K, T, S, H, N = 1024, 2048, 1024, 512, 256
FLOPS = 2 * (2 * K * H * S + H * N * S)

F32 = mybir.dt.float32
BF16 = mybir.dt.bfloat16
I32 = mybir.dt.int32
U32 = mybir.dt.uint32
U16 = mybir.dt.uint16
U8 = mybir.dt.uint8
FP8X4 = mybir.dt.float8_e4m3fn_x4
COPY = mybir.ActivationFunctionType.Copy
RELU = mybir.ActivationFunctionType.Relu
ADD = mybir.AluOpType.add

P = 128
PACK = 4
PASSES = K // (P * PACK)
HALF = S // 2
SPARE = 16
STRIPE = 16


def tile_picked_hub_relu_p_kernel(
    tc, x_words, x_scales, w1, w2, w3, offs, src, dst, out
):
    nc = tc.nc
    with ExitStack() as ctx:
        lists = ctx.enter_context(tc.tile_pool(name="lists", bufs=1))
        keep = ctx.enter_context(tc.tile_pool(name="keep", bufs=1))
        psum = ctx.enter_context(tc.psum_pool(name="psum", bufs=8))

        def sb(shape, dtype, name, tag=None):
            return keep.tile(shape, dtype, name=name, tag=tag or name, align_bytes=64)

        def entries(list_tile, first, count):
            return list_tile[:, first // STRIPE : (first + count) // STRIPE]

        offs_sb = lists.tile([P, S // STRIPE], U16, name="offs_sb")
        src_sb = lists.tile([P, S // STRIPE], U16, name="src_sb")
        dst_sb = lists.tile([P, S // STRIPE], U16, name="dst_sb")

        x_scale_table = sb([P, T], U8, "x_scale_table")
        nc.vector.memset(x_scale_table[:].bitcast(I32), 0)
        nc.sync.dma_start(offs_sb[:], offs)
        x_scale_rows = sb([P, T], U8, "x_scale_rows")
        for q in range(4):
            rows = slice(32 * q, 32 * q + 4 * PASSES)
            nc.sync.dma_start(
                out=x_scale_rows[rows, :].bitcast(I32),
                in_=x_scales[:, 4 * q : 4 * q + 4, :].bitcast(I32),
            )
            nc.vector.tensor_copy(x_scale_table[rows, :].bitcast(I32), x_scale_rows[rows, :].bitcast(I32))

        def load_words(g):
            table = sb([P, T], U32, f"x_word_table{g}")
            words = x_words[g].rearrange("p c r -> p (c r)").bitcast(I32)
            nc.sync.dma_start(out=table[:].bitcast(I32), in_=words)
            return table

        def load_pass(w, g, name, pieces=1):
            raw = sb([P, PACK * H], F32, name)
            rows = w[P * PACK * g : P * PACK * (g + 1), :].rearrange("(p j) c -> p (j c)", j=PACK)
            width = PACK * H // pieces
            for c in range(0, PACK * H, width):
                nc.sync.dma_start(out=raw[:, c : c + width], in_=rows[:, c : c + width])
            return raw

        x_word_table = [load_words(0)]
        w1_raw = [load_pass(w1, 0, "w1_raw0")]
        x_word_table.append(load_words(1))
        w1_raw.append(load_pass(w1, 1, "w1_raw1", pieces=2))
        nc.sync.dma_start(src_sb[:], src)
        w2_raw = [load_pass(w2, g, f"w2_raw{g}") for g in range(PASSES)]
        nc.sync.dma_start(dst_sb[:], dst)
        w3_raw = sb([P, PACK, N], F32, "w3_raw")
        w3_rows = w3.rearrange("(m t r) n -> t m r n", t=PACK, r=4)
        for t in range(PACK):
            nc.sync.dma_start(out=w3_raw[:, t, :], in_=w3_rows[t])

        x_scale = sb([P, S], U8, "x_scale")
        nc.vector.tensor_copy(x_scale[:], x_scale_table[:].indirect(offs_sb[:]))

        def pick_words(g, tag=None):
            codes = sb([P, S], U32, f"x_codes{g}", tag)
            nc.vector.tensor_copy(codes[:], x_word_table[g][:].indirect(offs_sb[:]))
            return codes

        x_codes = [pick_words(0)]

        def round_plane(copy, rounded, raw, t):
            copy(
                rounded.rearrange("p (m r j) -> p m j r", r=4, j=PACK),
                raw[:].rearrange("p (j m t r) -> p t m j r", j=PACK, t=PACK, r=4)[:, t],
            )

        def round_scalar(rounded, raw, t):
            round_plane(nc.scalar.copy, rounded, raw, t)

        def round_row_pair(rounded, raw, t, u):
            nc.scalar.copy(
                rounded.rearrange("p (m r u v) -> p u m v r", r=4, u=2, v=2)[:, u],
                raw[:, u * 2 * H : (u + 1) * 2 * H].rearrange("p (v m t r) -> p t m v r", v=2, t=PACK, r=4)[:, t],
            )

        def round_w1(name, g, planes):
            rounded = sb([P, len(planes) * H], BF16, name)
            for n, t in enumerate(planes):
                round_scalar(rounded[:, n * H : (n + 1) * H], w1_raw[g], t)
            return rounded

        def quantize(rounded, name):
            width = rounded.shape[1] // PACK
            codes = sb([P, width], U32, name + "_codes")
            scales = sb([P, width], U8, name + "_scales")
            nc.vector.quantize_mx(out=codes[:].bitcast(FP8X4), scales=scales[:], in_=rounded[:, :])
            return [(codes[:, c : c + P], scales[:, c : c + P]) for c in range(0, width, P)]

        def multiply(banks, weights, g):
            width = S // len(banks)
            for n, bank in enumerate(banks):
                nc.tensor.matmul_mx(
                    out=bank[:],
                    lhsT=weights[0].bitcast(FP8X4),
                    lhsT_scale=weights[1],
                    rhs=x_codes[g][:, n * width : (n + 1) * width].bitcast(FP8X4),
                    rhs_scale=x_scale[4 * g : P, n * width : (n + 1) * width],
                    start=(g == 0),
                    stop=(g == PASSES - 1),
                )

        def new_banks(count=2):
            return [psum.tile([P, S // count], F32, name="bank") for n in range(count)]

        def empty(banks, target, copies=(nc.scalar.copy, nc.scalar.copy)):
            width = S // len(banks)
            for n, bank in enumerate(banks):
                copies[n % 2](target[:, n * width : (n + 1) * width], bank[:])
            return target

        y_banks = []

        def open_plane(weights, count=2):
            y_banks.append(new_banks(count))
            multiply(y_banks[-1], weights, 0)

        opening = quantize(round_w1("w1_pass0_planes01", 0, (0, 1)), "w1_pass0_planes01")
        open_plane(opening[0], count=4)
        open_plane(opening[1])
        open_plane(quantize(round_w1("w1_pass0_plane2", 0, (2,)), "w1_pass0_plane2")[0])
        x_codes.append(pick_words(1, "w1_pass0_plane2"))

        plane3_pass0 = quantize(round_w1("w1_pass0_plane3", 0, (3,)), "w1_pass0_plane3")[0]
        rounded0 = sb([P, H], BF16, "w1_pass1_plane0")
        for u in range(2):
            round_row_pair(rounded0[:], w1_raw[1], 0, u)
        rounded1 = round_w1("w1_pass1_plane1", 1, (1,))
        rounded2 = round_w1("w1_pass1_plane2", 1, (2,))
        multiply(y_banks[0], quantize(rounded0, "w1_pass1_plane0")[0], 1)
        rounded3 = sb([P, H], BF16, "w1_pass1_plane3", "w1_pass1_plane0")
        round_plane(nc.vector.tensor_copy, rounded3[:], w1_raw[1], 3)
        multiply(y_banks[1], quantize(rounded1, "w1_pass1_plane1")[0], 1)
        y = [sb([P, S + SPARE if t == 1 else S], F32, f"y{t}") for t in range(PACK - 1)]
        e = [sb([P, S + SPARE if t < 2 else S], F32, f"e{t}") for t in range(PACK)]
        for window in (y[1], e[0], e[1]):
            nc.gpsimd.memset(window[:, S : S + SPARE], 0.0)
        on_scalar = (nc.scalar.copy, nc.scalar.copy)
        empty(y_banks[0], y[0], (nc.vector.tensor_copy, nc.scalar.copy))
        multiply(y_banks[2], quantize(rounded2, "w1_pass1_plane2")[0], 1)
        open_plane(plane3_pass0)
        multiply(y_banks[3], quantize(rounded3, "w1_pass1_plane3")[0], 1)

        y_picked = [[] for t in range(PACK)]

        def pick_y(t, first, count, picked, engine="scalar"):
            window = y[t][:].indirect(entries(src_sb, first, count))
            if engine == "scalar":
                nc.scalar.activation(picked, window, COPY)
            else:
                nc.vector.tensor_copy(picked, window)
            y_picked[t].append((first, picked))

        def round_w2(rounded, g, planes):
            first = planes[0]
            nc.vector.tensor_copy(
                rounded.rearrange("p (t m r j) -> p t m j r", t=len(planes), r=4, j=PACK),
                w2_raw[g][:].rearrange("p (j m t r) -> p t m j r", j=PACK, t=PACK, r=4)[:, first : first + len(planes)],
            )
            return rounded

        picked0 = sb([P, S], F32, "y_picked0")
        pick_y(0, 0, HALF, picked0[:, 0:HALF], "vector")
        empty(y_banks[1], y[1], on_scalar)
        w2_pass0_01 = round_w2(sb([P, 2 * H], BF16, "w2_pass0_planes01")[:, :], 0, (0, 1))
        empty(y_banks[2], y[2], on_scalar)
        pick_y(0, HALF, HALF, picked0[:, HALF:S])
        y_picked[0] = [(0, picked0[:, :])]
        pick_y(1, 0, S, sb([P, S], F32, "y_picked1")[:, :])
        w2_23 = sb([P, 4 * H], BF16, "w2_planes23")
        round_w2(w2_23[:, 0 : 2 * H], 0, (2, 3))
        weights = quantize(w2_pass0_01, "w2_pass0_planes01")
        e_banks = [new_banks() for t in range(2)]
        for t in range(2):
            multiply(e_banks[t], weights[t], 0)
        w2_pass1_0 = round_w2(sb([P, H], BF16, "w2_pass1_plane0")[:, :], 1, (0,))
        w2_pass1_1 = round_w2(sb([P, H], BF16, "w2_pass1_plane1")[:, :], 1, (1,))
        multiply(e_banks[0], quantize(w2_pass1_0, "w2_pass1_plane0")[0], 1)
        multiply(e_banks[1], quantize(w2_pass1_1, "w2_pass1_plane1")[0], 1)
        round_w2(w2_23[:, 2 * H : 4 * H], 1, (2, 3))
        weights = quantize(w2_23, "w2_planes23")
        empty(e_banks[0], e[0], on_scalar)
        y.append(sb([P, S], F32, "y3", "w2_pass1_plane0_codes"))
        empty(y_banks[3], y[3], on_scalar)
        empty(e_banks[1], e[1], on_scalar)
        for t in range(2):
            e_banks.append(new_banks())
            multiply(e_banks[-1], weights[t], 0)
            multiply(e_banks[-1], weights[2 + t], 1)

        sums = sb([P, PACK * S], F32, "sums", "w3_raw")

        def add(t, first, count):
            piece, picked = [entry for entry in y_picked[t] if entry[0] <= first][-1]
            nc.vector.tensor_tensor(
                sums[:, t * S + first : t * S + first + count],
                e[t][:].indirect(entries(dst_sb, first, count)),
                picked[:, first - piece : first - piece + count],
                ADD,
            )

        w3_rounded = w2_23[:, 0 : PACK * N]
        nc.vector.tensor_copy(
            w3_rounded.rearrange("p (c r t) -> p c t r", r=4, t=PACK),
            w3_raw[:].rearrange("p t (c r) -> p c t r", r=4),
        )
        pick_y(2, 0, HALF, sb([P, HALF], F32, "y_picked20", "w2_pass1_plane1")[:, :], "vector")
        w3_mx = quantize(w3_rounded, "w3")
        empty(e_banks[2], e[2], on_scalar)
        pick_y(3, 0, HALF, sb([P, HALF], F32, "y_picked30")[:, :])
        empty(e_banks[3], e[3], on_scalar)
        for t in range(2):
            add(t, 0, S)
        for t in range(2, PACK):
            add(t, 0, HALF)

        out_rows = out.rearrange("(m p) r -> p m r", p=P)
        z_rounded, out_bank = {}, {}

        def relu(first, count, engine, rounded=None):
            z_rounded[first] = sb([P, PACK * count], BF16, f"z{first}")[:, :] if rounded is None else rounded
            target = z_rounded[first].rearrange("p (c r t) -> p c t r", r=4, t=PACK)
            source = sums[:].rearrange("p (t c r) -> p c t r", t=PACK, r=4)[:, first // 4 : (first + count) // 4]
            if engine == "scalar":
                nc.scalar.activation(target, source, RELU)
            else:
                nc.vector.tensor_scalar_max(target, source, 0.0)

        def last_product(first):
            count = z_rounded[first].shape[1] // PACK
            z_codes = sb([P, count], U32, f"z_codes{first}")
            z_scales = sb([P, count], U8, f"z_scales{first}")
            nc.vector.quantize_mx(out=z_codes[:].bitcast(FP8X4), scales=z_scales[:], in_=z_rounded[first])
            out_bank[first] = psum.tile([P, N // P, count], F32, name="bank")
            for m in range(N // P):
                nc.tensor.matmul_mx(
                    out=out_bank[first][:, m, :],
                    lhsT=w3_mx[m][0].bitcast(FP8X4),
                    lhsT_scale=w3_mx[m][1],
                    rhs=z_codes[:].bitcast(FP8X4),
                    rhs_scale=z_scales[:],
                    start=True,
                    stop=True,
                )

        def store(first, copy=nc.scalar.copy):
            count = out_bank[first].shape[2]
            result = sb([P, N // P, count], F32, f"result{first}")
            copy(result[:], out_bank[first][:])
            nc.sync.dma_start(out=out_rows[:, :, first : first + count], in_=result[:])

        late23 = sb([P, S], F32, "y_late23", "w1_pass0_plane2")
        pick_y(2, HALF, HALF, late23[:, 0:HALF])
        pick_y(3, HALF, HALF, late23[:, HALF:S])
        relu(0, 256, "scalar")
        add(2, 512, 256)
        relu(256, 256, "vector")
        add(3, 512, 256)
        relu(512, 256, "scalar")
        last_product(256)
        add(2, 768, 256)
        last_product(0)
        add(3, 768, 256)
        store(256)
        store(0)
        last_product(512)
        relu(768, 128, "vector", sums[:, 512:768].bitcast(BF16))
        relu(896, 128, "vector", sums[:, S + 512 : S + 768].bitcast(BF16))
        last_product(768)
        last_product(896)
        store(512)
        store(768)
        store(896, nc.vector.tensor_copy)
